import numpy as np
import ml_dtypes


def mxq(x, axis, fmt="e4m3"):
    dtype, down = {"e4m3": (ml_dtypes.float8_e4m3fn, 7), "e5m2": (ml_dtypes.float8_e5m2, 14)}[fmt]
    v = np.moveaxis(np.asarray(x, np.float32).astype(ml_dtypes.bfloat16).astype(np.float64), axis, -1)
    blocks = v.reshape(v.shape[:-1] + (-1, 32))
    amax = np.abs(blocks).max(-1, keepdims=True)
    byte = np.maximum(np.where(amax > 0, np.frexp(amax)[1] - 1 + 127, 0) - down, 1)
    scale = np.exp2(byte - 127.0)
    codes = (blocks / scale).astype(np.float32).astype(dtype).astype(np.float64)
    return np.moveaxis((codes * scale).reshape(v.shape), -1, axis)


WIDE = False


def mx_kscale(k):
    if not WIDE:
        return np.ones(k)
    levels = np.array([10, -10, 5, -5, 0])
    if k % 512:
        return np.exp2(np.random.permutation(np.resize(levels, k // 32))).repeat(32)
    a = np.empty((k // 512, 16))
    for p in range(k // 512):
        a[p, :8] = np.random.permutation(np.resize(levels, 8))
        for g in range(8):
            far = levels[np.abs(levels - a[p, g]) >= 10]
            a[p, g + 8] = far[np.random.randint(len(far))]
    return np.exp2(a.ravel()).repeat(32)


BF16 = ml_dtypes.bfloat16


def bf(x):
    return np.asarray(x, np.float32).astype(BF16)


def f64(x):
    return np.asarray(x).astype(np.float64)


E2M1 = np.array([0.0, 0.5, 1.0, 1.5, 2.0, 3.0, 4.0, 6.0, -0.0, -0.5, -1.0, -1.5, -2.0, -3.0, -4.0, -6.0])


def pack_weight(w, fmt):
    k, n = w.shape
    w = f64(bf(w)).reshape(k // 32, 32, n)
    amax = np.abs(w).max(1)
    if fmt == "e4m3":
        byte = np.frexp(amax)[1] - 1 + 127 - 7
    else:
        mant, ex = np.frexp(amax / 6.0)
        byte = np.where(mant > 0.5, ex, ex - 1) + 127
    byte = np.clip(np.where(amax > 0, byte, 1), 1, 254)
    scaled = (w * np.exp2(127.0 - byte)[:, None, :]).reshape(k, n).astype(np.float32)
    by_word = np.ascontiguousarray(scaled.reshape(k // 512, 128, 4, n).transpose(0, 1, 3, 2))
    if fmt == "e4m3":
        words = by_word.astype(ml_dtypes.float8_e4m3fn).view(np.uint8)
    else:
        c = by_word.astype(ml_dtypes.float4_e2m1fn).view(np.uint8) & 0xF
        words = c[..., 0::2] | (c[..., 1::2] << 4)
    return np.ascontiguousarray(words), np.ascontiguousarray(byte.astype(np.uint8).reshape(k // 512, 16, n))


def unpack_weight(words, scales, fmt):
    g, p, n, _ = words.shape
    if fmt == "e4m3":
        vals = np.ascontiguousarray(words).view(ml_dtypes.float8_e4m3fn).astype(np.float64)
    else:
        nib = np.empty((g, p, n, 4), np.uint8)
        nib[..., 0::2] = words & 0xF
        nib[..., 1::2] = words >> 4
        vals = E2M1[nib]
    vals = vals * np.repeat(np.exp2(scales.astype(np.float64) - 127.0), 8, axis=1)[..., None]
    return vals.transpose(0, 1, 3, 2).reshape(g * 512, n)
def pack4(w):
    words, scales = pack_weight(w, "e2m1")
    return words.reshape(words.shape[0], 128, -1), scales


def unpack4(words, scales):
    return unpack_weight(words.reshape(words.shape[0], 128, -1, 2), scales, "e2m1")


C, G, D = 1024, 1024, 2048


def setup_inputs():
    s, t = mx_kscale(C), mx_kscale(G)
    x = np.random.standard_normal((C, G)) * s[:, None] * t
    a = np.random.standard_normal((C, C)) / (3 * np.sqrt(C)) / s[:, None] * s
    b = np.random.standard_normal((G, G)) / (3 * np.sqrt(G)) / t[:, None] * t
    e = np.random.standard_normal((C, D)) / np.sqrt(C) / s[:, None]
    gain = (1 + 0.1 * np.random.standard_normal(G)) / t
    y = np.random.standard_normal((D, G))
    a_words, a_scales = pack4(a)
    b_words, b_scales = pack4(b)
    e_words, e_scales = pack4(e)
    return {"x": bf(x), "a_words": a_words, "a_scales": a_scales,
            "b_words": b_words, "b_scales": b_scales, "gain": bf(gain),
            "e_words": e_words, "e_scales": e_scales, "y": bf(y)}


def reference(x, a_words, a_scales, b_words, b_scales, gain, e_words, e_scales, y):
    a = unpack4(a_words, a_scales)
    b = unpack4(b_words, b_scales)
    e = unpack4(e_words, e_scales)
    x = f64(x)
    h1 = x + (a.T @ mxq(x, 0, "e4m3"))
    h2 = (h1 + (mxq(h1, 1, "e4m3") @ b)) * f64(gain)
    return f64(y) + (e.T @ mxq(h2, 0, "e4m3"))

@@ -1,0 +1,379 @@
+from contextlib import ExitStack
+
+import concourse.mybir as mybir
+from concourse.masks import make_identity
+
+C, G, D = 1024, 1024, 2048
+FLOPS = 2 * C * C * G + 2 * C * G * G + 2 * C * D * G
+
+F32 = mybir.dt.float32
+BF16 = mybir.dt.bfloat16
+I32 = mybir.dt.int32
+U32 = mybir.dt.uint32
+U8 = mybir.dt.uint8
+FP8X4 = mybir.dt.float8_e4m3fn_x4
+FP4X4 = mybir.dt.float4_e2m1fn_x4
+ADD = mybir.AluOpType.add
+MULT = mybir.AluOpType.mult
+
+P = 128
+S_BLOCKS = ((0, 2), (0, 3), (1, 3))
+G_EVERY = 4
+
+
+def tile_anchor_offset_transfer_t2_kernel(
+    tc, x, a_words, a_scales, b_words, b_scales, gain, e_words, e_scales, y, out
+):
+    nc = tc.nc
+    with ExitStack() as ctx:
+        keep = ctx.enter_context(tc.tile_pool(name="keep", bufs=1))
+        psum = ctx.enter_context(tc.psum_pool(name="psum", bufs=8))
+        ctx.enter_context(tc.manual_schedule())
+
+        def sb(name, shape, dtype, tag=None, bufs=1):
+            return keep.tile(shape, dtype, name=name, tag=tag or name, bufs=bufs, align_bytes=256)
+
+        def bank(name, shape):
+            return psum.tile(shape, F32, name=name, tag="bank", bufs=8)
+
+        a_w = sb("a_w", [P, 2, 2 * C], U8)
+        a_s = sb("a_s", [P, 2, C], U8)
+        b_raw = sb("b_raw", [P, 2, 2 * G], U8)
+        bs_raw = sb("bs_raw", [P, 2, G], U8)
+        b_w = sb("b_w", [P, 2, 2 * G], U8)
+        b_s = sb("b_s", [P, 2, G], U8)
+        e_w = sb("e_w", [P, 2, 2 * D], U8)
+        e_s = sb("e_s", [P, 2, D], U8)
+        xq = sb("xq", [P, 2, G], U32)
+        xs = sb("xs", [P, 2, G], U8)
+        x_t = sb("x_t", [P, 2, C, 4], BF16)
+        h1f = sb("h1f", [P, 2, C, 4], F32)
+        h1g = sb("h1g", [P, 2, 4, 2, 512], F32)
+        h1q = sb("h1q", [P, 2, C], U32)
+        h1s = sb("h1s", [P, 2, C], U8)
+        h2q = sb("h2q", [P, 2, G], U32)
+        h2s = sb("h2s", [P, 2, G], U8)
+        y_sb = sb("y_sb", [P, D // P, G], BF16)
+        gain_b = sb("gain_b", [P, 2, 4], BF16)
+        gain_f = sb("gain_f", [P, 2, 4], F32)
+        ident = sb("ident", [P, P], F32)
+        warm = sb("warm", [P, 8], F32)
+        x_raw = [sb("x_raw%d" % h, [P, 2, 4, 512], BF16, tag="r1", bufs=2) for h in range(2)]
+        xi = [sb("xi%d" % h, [P, 2, 4, P, 4], BF16, tag="r2", bufs=2) for h in range(2)]
+
+        nc.vector.memset(a_s[:].bitcast(I32), 0)
+        nc.vector.memset(warm[:], 0.0)
+        nc.vector.memset(bs_raw[:].bitcast(I32), 0)
+        nc.vector.memset(e_s[:].bitcast(I32), 0)
+        nc.scalar.copy(out=warm[:, 4:5], in_=warm[:, 0:1])
+        make_identity(nc, ident[:])
+
+        x_v = x.rearrange("(k p j) w -> k p j w", k=2, p=P)
+
+        def load_x(h):
+            for k in range(2):
+                nc.sync.dma_start(out=x_raw[h][:, k, :, :], in_=x_v[k][:, :, 512 * h : 512 * h + 512])
+
+        def load_scales(dst, src):
+            s_v = src.rearrange("k (q r) n -> r q k n", r=4)
+            for r in range(4):
+                nc.sync.dma_start(out=dst[r:P:32, :, :].bitcast(I32), in_=s_v[r].bitcast(I32))
+
+        def load_words(dst, src):
+            nc.sync.dma_start(out=dst[:].bitcast(I32), in_=src.rearrange("k p n -> p k n").bitcast(I32))
+
+        load_x(0)
+        load_scales(a_s, a_scales)
+        load_words(a_w, a_words)
+        load_x(1)
+        load_words(b_raw, b_words)
+        load_scales(bs_raw, b_scales)
+        nc.sync.dma_start(out=gain_b[:], in_=gain.rearrange("(a m t) -> m a t", m=P, t=4))
+        load_words(e_w, e_words)
+        load_scales(e_s, e_scales)
+        y_v = y.rearrange("(i p) g -> p i g", p=P)
+        for i in range(0, D // P, 4):
+            nc.sync.dma_start(out=y_sb[:, i : i + 4, :], in_=y_v[:, i : i + 4, :])
+        nc.gpsimd.tensor_copy(out=gain_f[:], in_=gain_b[:])
+
+        def xi_block(h, k, t0, n, engine_copy):
+            v = x_raw[h][:, k, :, :].rearrange("p j (m t) -> p t m j", t=4)
+            engine_copy(out=xi[h][:, k, t0 : t0 + n, :, :], in_=v[:, t0 : t0 + n, :, :])
+
+        def xi_scalar(h):
+            for k, t in S_BLOCKS:
+                xi_block(h, k, t, 1, nc.scalar.copy)
+
+        def xi_vector(h):
+            for k in range(2):
+                for t in range(4):
+                    if (k, t) not in S_BLOCKS:
+                        xi_block(h, k, t, 1, nc.vector.tensor_copy)
+
+        def x_quant(h):
+            for k in range(2):
+                nc.vector.quantize_mx(
+                    out=xq[:, k, 512 * h : 512 * h + 512].bitcast(FP8X4),
+                    scales=xs[:, k, 512 * h : 512 * h + 512],
+                    in_=xi[h][:, k, :, :, :].rearrange("p t m j -> p (t m j)"),
+                )
+
+        def x_transpose(h):
+            words = x_raw[h][:].rearrange("p k j w -> p (k j w)").bitcast(F32)
+            banks = []
+            for k in range(2):
+                for jp in range(2):
+                    b = bank("xt%d%d%d" % (h, k, jp), [P, 2, 2, P])
+                    for jj in range(2):
+                        base = (4 * k + 2 * jp + jj) * 256
+                        for u in range(2):
+                            nc.tensor.transpose(b[:, jj, u, :], words[:, base + u : base + 256 : 2], ident[:])
+                    banks.append((k, jp, b))
+            return banks
+
+        def x_empty(h, banks):
+            words = x_t[:].rearrange("m a c t -> m (a c t)").bitcast(F32)
+            for k, jp, b in banks:
+                base = (1024 * h + 512 * k) * 2
+                dst = words[:, base : base + 1024].rearrange("m (p j u) -> m p j u", j=4, u=2)
+                nc.scalar.copy(out=dst[:, :, 2 * jp : 2 * jp + 2, :], in_=b[:].rearrange("m j u p -> m p j u"))
+
+        def s1_mm(h, ch):
+            b = bank("s1_%d_%d" % (h, ch), [P, 4, P])
+            for t in range(4):
+                w = 512 * h + P * t
+                for k in range(2):
+                    nc.tensor.matmul_mx(
+                        out=b[:, t, :],
+                        lhsT=xq[:, k, w : w + P].bitcast(FP8X4),
+                        lhsT_scale=xs[:, k, w : w + P],
+                        rhs=a_w[:, k, 2 * P * ch : 2 * P * (ch + 1)].bitcast(FP4X4),
+                        rhs_scale=a_s[:, k, P * ch : P * (ch + 1)],
+                        start=(k == 0),
+                        stop=(k == 1),
+                    )
+            return b
+
+        def s1_add(h, ch, b):
+            cols = slice(P * ch, P * (ch + 1))
+            nc.vector.tensor_tensor(
+                out=h1f[:, h, cols, :], in0=b[:].rearrange("m t c -> m c t"), in1=x_t[:, h, cols, :], op=ADD
+            )
+
+        h1b = {}
+
+        def h1_round(h, ch):
+            hc, cc = divmod(ch, 4)
+            if cc == 0:
+                h1b[h, hc] = sb("h1b%d%d" % (h, hc), [P, 512, 4], BF16, tag="h1b", bufs=2)
+            dst = h1b[h, hc][:].rearrange("m (u p e) t -> m u p (e t)", u=2, e=2)
+            src = h1f[:, h, P * ch : P * (ch + 1), :].rearrange("m (p u e) t -> m u p (e t)", u=2, e=2)
+            nc.scalar.copy(out=dst[:, :, 32 * cc : 32 * cc + 32, :], in_=src)
+
+        def h1_quant(h, hc):
+            nc.vector.quantize_mx(
+                out=h1q[:, h, 512 * hc : 512 * hc + 512].bitcast(FP8X4),
+                scales=h1s[:, h, 512 * hc : 512 * hc + 512],
+                in_=h1b[h, hc][:].rearrange("m c t -> m (c t)"),
+            )
+
+        def h1_gain(a, hc):
+            for t in range(4):
+                v = h1f[:, a, 512 * hc : 512 * hc + 512, t].rearrange("m (p u e) -> m u p e", u=2, e=2)
+                nc.gpsimd.tensor_scalar(
+                    out=h1g[:, a, t, hc, :].rearrange("m (u p e) -> m u p e", u=2, e=2),
+                    in0=v,
+                    scalar1=gain_f[:, a, t : t + 1],
+                    scalar2=0.0,
+                    op0=MULT,
+                    op1=ADD,
+                )
+
+        def b_permute(a):
+            for k in range(2):
+                nc.vector.tensor_copy(
+                    out=b_w[:, k, 1024 * a : 1024 * a + 1024].rearrange("p (t m b) -> p t m b", t=4, b=2),
+                    in_=b_raw[:, k, 1024 * a : 1024 * a + 1024].rearrange("p (m t b) -> p t m b", t=4, b=2),
+                )
+                nc.vector.tensor_copy(
+                    out=b_s[:, k, 512 * a : 512 * a + 512].rearrange("p (t m) -> p t m", t=4),
+                    in_=bs_raw[:, k, 512 * a : 512 * a + 512].rearrange("p (m t) -> p t m", t=4),
+                )
+
+        h2t = {}
+        h2i = {}
+
+        def s2_mm(a, hc, t):
+            b = bank("s2_%d%d%d" % (a, hc, t), [P, 512])
+            w = 512 * a + P * t
+            for k in range(2):
+                nc.tensor.matmul_mx(
+                    out=b[:],
+                    lhsT=b_w[:, k, 2 * w : 2 * w + 2 * P].bitcast(FP4X4),
+                    lhsT_scale=b_s[:, k, w : w + P],
+                    rhs=h1q[:, k, 512 * hc : 512 * hc + 512].bitcast(FP8X4),
+                    rhs_scale=h1s[:, k, 512 * hc : 512 * hc + 512],
+                    start=(k == 0),
+                    stop=(k == 1),
+                )
+            return b
+
+        def s2_add(a, hc, t, b):
+            if a not in h2t:
+                h2t[a] = sb("h2t%d" % a, [P, 4, 2, 512], BF16, tag="r2", bufs=2)
+            nc.vector.scalar_tensor_tensor(
+                out=h2t[a][:, t, hc, :],
+                in0=b[:],
+                scalar=gain_f[:, a, t : t + 1],
+                in1=h1g[:, a, t, hc, :],
+                op0=MULT,
+                op1=ADD,
+            )
+
+        def h2_transpose(a, hc):
+            words = h2t[a][:].rearrange("m t k c -> m (t k c)").bitcast(F32)
+            banks = []
+            for tp in range(2):
+                b = bank("ht%d%d%d" % (a, hc, tp), [P, 2, 2, P])
+                for tt in range(2):
+                    base = ((2 * tp + tt) * 2 + hc) * 256
+                    for u in range(2):
+                        nc.tensor.transpose(b[:, tt, u, :], words[:, base + P * u : base + P * (u + 1)], ident[:])
+                banks.append((tp, b))
+            return banks
+
+        def h2_empty(a, hc, banks):
+            if a not in h2i:
+                h2i[a] = sb("h2i%d" % a, [P, 2, 512, 4], BF16, tag="r1", bufs=2)
+            words = h2i[a][:].rearrange("p k g j -> p (k g j)").bitcast(F32)
+            for tp, b in banks:
+                base = (hc * 512 + tp * 256) * 2
+                nc.scalar.copy(
+                    out=words[:, base : base + 512].rearrange("p (t m u) -> p t m u", t=2, u=2),
+                    in_=b[:].rearrange("p t u m -> p t m u"),
+                )
+
+        def h2_quant(a, hc):
+            nc.vector.quantize_mx(
+                out=h2q[:, hc, 512 * a : 512 * a + 512].bitcast(FP8X4),
+                scales=h2s[:, hc, 512 * a : 512 * a + 512],
+                in_=h2i[a][:, hc, :, :].rearrange("p g j -> p (g j)"),
+            )
+
+        def s3_mm(a, i):
+            b = bank("s3_%d_%d" % (a, i), [P, 512])
+            for k in range(2):
+                nc.tensor.matmul_mx(
+                    out=b[:],
+                    lhsT=e_w[:, k, 2 * P * i : 2 * P * (i + 1)].bitcast(FP4X4),
+                    lhsT_scale=e_s[:, k, P * i : P * (i + 1)],
+                    rhs=h2q[:, k, 512 * a : 512 * a + 512].bitcast(FP8X4),
+                    rhs_scale=h2s[:, k, 512 * a : 512 * a + 512],
+                    start=(k == 0),
+                    stop=(k == 1),
+                )
+            return b
+
+        def s3_add(a, i, b):
+            o = sb("o_%d_%d" % (a, i), [P, P, 4], F32, tag="o", bufs=6)
+            y_cols = y_sb[:, i, 512 * a : 512 * a + 512].rearrange("p (m t) -> p m t", t=4)
+            b_cols = b[:].rearrange("p (t m) -> p m t", t=4)
+            if (16 * a + i) % G_EVERY == G_EVERY - 1 and 16 * a + i < 30:
+                s = sb("s_%d_%d" % (a, i), [P, P, 4], F32, tag="s", bufs=2)
+                nc.scalar.copy(out=s[:], in_=b_cols)
+                nc.gpsimd.tensor_tensor(out=o[:], in0=s[:], in1=y_cols, op=ADD)
+                return (True, a, i, o)
+            nc.vector.tensor_tensor(out=o[:], in0=b_cols, in1=y_cols, op=ADD)
+            return (False, a, i, o)
+
+        def store(item):
+            slow, a, i, o = item
+            nc.sync.dma_start(
+                out=out[P * i : P * (i + 1), 512 * a : 512 * a + 512], in_=o[:].rearrange("p m t -> p (m t)")
+            )
+
+        xi_scalar(0)
+        xi_vector(0)
+        tr = x_transpose(0)
+        x_quant(0)
+        x_empty(0, tr)
+        for ch in range(3):
+            s1_add(0, ch, s1_mm(0, ch))
+        b3 = s1_mm(0, 3)
+        xi_scalar(1)
+        xi_vector(1)
+        tr = x_transpose(1)
+        s1_add(0, 3, b3)
+        x_quant(1)
+        h1_round(0, 0)
+        x_empty(1, tr)
+        for ch in range(1, 4):
+            h1_round(0, ch)
+        h1_gain(0, 0)
+        for ch in range(4, 8):
+            s1_add(0, ch, s1_mm(0, ch))
+            h1_round(0, ch)
+            if ch == 5:
+                h1_quant(0, 0)
+        b_permute(0)
+        h1_gain(0, 1)
+        for ch in range(8):
+            s1_add(1, ch, s1_mm(1, ch))
+            h1_round(1, ch)
+            if ch == 0:
+                h1_quant(0, 1)
+            if ch == 3:
+                h1_gain(1, 0)
+            if ch == 4:
+                b_permute(1)
+            if ch == 5:
+                h1_quant(1, 0)
+        h1_gain(1, 1)
+        for t in range(4):
+            s2_add(0, 0, t, s2_mm(0, 0, t))
+            if t == 1:
+                h1_quant(1, 1)
+        b01 = [s2_mm(0, 1, t) for t in range(4)]
+        tr00 = h2_transpose(0, 0)
+        h2_empty(0, 0, tr00)
+        for t in range(4):
+            s2_add(0, 1, t, b01[t])
+        b10 = [s2_mm(1, 0, t) for t in range(2)]
+        tr01 = h2_transpose(0, 1)
+        b10 += [s2_mm(1, 0, t) for t in range(2, 4)]
+        h2_empty(0, 1, tr01)
+        h2_quant(0, 0)
+        s2_add(1, 0, 0, b10[0])
+        s2_add(1, 0, 1, b10[1])
+        h2_quant(0, 1)
+        s2_add(1, 0, 2, b10[2])
+        s2_add(1, 0, 3, b10[3])
+        b11 = [s2_mm(1, 1, t) for t in range(4)]
+        tr10 = h2_transpose(1, 0)
+        h2_empty(1, 0, tr10)
+        for t in range(4):
+            s2_add(1, 1, t, b11[t])
+        late = []
+
+        def out_step(n, b):
+            a, i = divmod(n, 16)
+            item = s3_add(a, i, b)
+            if item[0]:
+                late.append((n, item))
+            else:
+                store(item)
+            while late and n - late[0][0] >= 3:
+                store(late.pop(0)[1])
+
+        s3 = {}
+        for n in range(2):
+            s3[n] = s3_mm(0, n)
+        tr11 = h2_transpose(1, 1)
+        h2_empty(1, 1, tr11)
+        h2_quant(1, 0)
+        for n in range(32):
+            if n not in s3:
+                s3[n] = s3_mm(n // 16, n % 16)
+            out_step(n, s3[n])
+            if n == 1:
+                h2_quant(1, 1)

@@ -17,8 +17,17 @@ ADD = mybir.AluOpType.add
 MULT = mybir.AluOpType.mult
 
 P = 128
-S_BLOCKS = ((0, 2), (0, 3), (1, 3))
-G_EVERY = 4
+V_BLOCKS = ((2, 3), (1, 1))
+G_BLOCKS = 0
+G_RD = ()
+G_HS = ()
+G_BP = ()
+G_ADD = ()
+G_OUT = ()
+LOADS = ('x00', 'x01', 'g', 'as', 'aw', 'x10', 'x11', 'bw', 'bs')
+O_BUFS = 8
+G_LAG = 2.5
+XE_AT = 0
 
 
 def tile_anchor_offset_transfer_t2_kernel(
@@ -48,7 +57,6 @@ def tile_anchor_offset_transfer_t2_kernel(
         xs = sb("xs", [P, 2, G], U8)
         x_t = sb("x_t", [P, 2, C, 4], BF16)
         h1f = sb("h1f", [P, 2, C, 4], F32)
-        h1g = sb("h1g", [P, 2, 4, 2, 512], F32)
         h1q = sb("h1q", [P, 2, C], U32)
         h1s = sb("h1s", [P, 2, C], U8)
         h2q = sb("h2q", [P, 2, G], U32)
@@ -70,10 +78,6 @@ def tile_anchor_offset_transfer_t2_kernel(
 
         x_v = x.rearrange("(k p j) w -> k p j w", k=2, p=P)
 
-        def load_x(h):
-            for k in range(2):
-                nc.sync.dma_start(out=x_raw[h][:, k, :, :], in_=x_v[k][:, :, 512 * h : 512 * h + 512])
-
         def load_scales(dst, src):
             s_v = src.rearrange("k (q r) n -> r q k n", r=4)
             for r in range(4):
@@ -82,61 +86,80 @@ def tile_anchor_offset_transfer_t2_kernel(
         def load_words(dst, src):
             nc.sync.dma_start(out=dst[:].bitcast(I32), in_=src.rearrange("k p n -> p k n").bitcast(I32))
 
-        load_x(0)
-        load_scales(a_s, a_scales)
-        load_words(a_w, a_words)
-        load_x(1)
-        load_words(b_raw, b_words)
-        load_scales(bs_raw, b_scales)
-        nc.sync.dma_start(out=gain_b[:], in_=gain.rearrange("(a m t) -> m a t", m=P, t=4))
+        def load_x_half(h, k):
+            nc.sync.dma_start(out=x_raw[h][:, k, :, :], in_=x_v[k][:, :, 512 * h : 512 * h + 512])
+
+        def load_gain():
+            nc.sync.dma_start(out=gain_b[:], in_=gain.rearrange("(a m t) -> m a t", m=P, t=4))
+            nc.gpsimd.tensor_copy(out=gain_f[:], in_=gain_b[:])
+
+        loads = {
+            "x00": lambda: load_x_half(0, 0),
+            "x01": lambda: load_x_half(0, 1),
+            "x10": lambda: load_x_half(1, 0),
+            "x11": lambda: load_x_half(1, 1),
+            "g": load_gain,
+            "as": lambda: load_scales(a_s, a_scales),
+            "aw": lambda: load_words(a_w, a_words),
+            "bs": lambda: load_scales(bs_raw, b_scales),
+            "bw": lambda: load_words(b_raw, b_words),
+        }
+        for step in LOADS:
+            loads[step]()
         load_words(e_w, e_words)
         load_scales(e_s, e_scales)
         y_v = y.rearrange("(i p) g -> p i g", p=P)
         for i in range(0, D // P, 4):
             nc.sync.dma_start(out=y_sb[:, i : i + 4, :], in_=y_v[:, i : i + 4, :])
-        nc.gpsimd.tensor_copy(out=gain_f[:], in_=gain_b[:])
 
         def xi_block(h, k, t0, n, engine_copy):
             v = x_raw[h][:, k, :, :].rearrange("p j (m t) -> p t m j", t=4)
             engine_copy(out=xi[h][:, k, t0 : t0 + n, :, :], in_=v[:, t0 : t0 + n, :, :])
 
-        def xi_scalar(h):
-            for k, t in S_BLOCKS:
-                xi_block(h, k, t, 1, nc.scalar.copy)
+        def xi_scalar(h, k):
+            n = V_BLOCKS[h][k]
+            if h == 1:
+                n += G_BLOCKS
+            if n < 4:
+                xi_block(h, k, n, 4 - n, nc.scalar.copy)
 
-        def xi_vector(h):
-            for k in range(2):
-                for t in range(4):
-                    if (k, t) not in S_BLOCKS:
-                        xi_block(h, k, t, 1, nc.vector.tensor_copy)
-
-        def x_quant(h):
-            for k in range(2):
-                nc.vector.quantize_mx(
-                    out=xq[:, k, 512 * h : 512 * h + 512].bitcast(FP8X4),
-                    scales=xs[:, k, 512 * h : 512 * h + 512],
-                    in_=xi[h][:, k, :, :, :].rearrange("p t m j -> p (t m j)"),
+        def xi_gpsimd(h, k):
+            n = V_BLOCKS[h][k]
+            v = x_raw[h][:, k, :, :].rearrange("p j (m t) -> p t m j", t=4)
+            for t in range(n, n + G_BLOCKS):
+                nc.gpsimd.tensor_scalar(
+                    out=xi[h][:, k, t, :, :], in0=v[:, t], scalar1=1.0, scalar2=0.0, op0=MULT, op1=ADD
                 )
 
-        def x_transpose(h):
-            words = x_raw[h][:].rearrange("p k j w -> p (k j w)").bitcast(F32)
-            banks = []
-            for k in range(2):
-                for jp in range(2):
-                    b = bank("xt%d%d%d" % (h, k, jp), [P, 2, 2, P])
-                    for jj in range(2):
-                        base = (4 * k + 2 * jp + jj) * 256
-                        for u in range(2):
-                            nc.tensor.transpose(b[:, jj, u, :], words[:, base + u : base + 256 : 2], ident[:])
-                    banks.append((k, jp, b))
-            return banks
+        def xi_vector(h, k):
+            n = V_BLOCKS[h][k]
+            if n % 2:
+                xi_block(h, k, n - 1, 1, nc.vector.tensor_copy)
+                n -= 1
+            if n:
+                xi_block(h, k, 0, n, nc.vector.tensor_copy)
 
-        def x_empty(h, banks):
+        def x_quant(h, k):
+            nc.vector.quantize_mx(
+                out=xq[:, k, 512 * h : 512 * h + 512].bitcast(FP8X4),
+                scales=xs[:, k, 512 * h : 512 * h + 512],
+                in_=xi[h][:, k, :, :, :].rearrange("p t m j -> p (t m j)"),
+            )
+
+        def x_transpose(h, k, jp):
+            words = x_raw[h][:].rearrange("p k j w -> p (k j w)").bitcast(F32)
+            b = bank("xt%d%d%d" % (h, k, jp), [P, 2, 2, P])
+            for jj in range(2):
+                base = (4 * k + 2 * jp + jj) * 256
+                for u in range(2):
+                    nc.tensor.transpose(b[:, jj, u, :], words[:, base + u : base + 256 : 2], ident[:])
+            return b
+
+        def x_empty(h, k, jp, b):
             words = x_t[:].rearrange("m a c t -> m (a c t)").bitcast(F32)
-            for k, jp, b in banks:
-                base = (1024 * h + 512 * k) * 2
-                dst = words[:, base : base + 1024].rearrange("m (p j u) -> m p j u", j=4, u=2)
-                nc.scalar.copy(out=dst[:, :, 2 * jp : 2 * jp + 2, :], in_=b[:].rearrange("m j u p -> m p j u"))
+            base = (1024 * h + 512 * k) * 2
+            dst = words[:, base : base + 1024].rearrange("m (p j u) -> m p j u", j=4, u=2)
+            nc.scalar.copy(out=dst[:, :, 2 * jp : 2 * jp + 2, :], in_=b[:].rearrange("m j u p -> m p j u"))
 
         def s1_mm(h, ch):
             b = bank("s1_%d_%d" % (h, ch), [P, 4, P])
@@ -160,15 +183,30 @@ def tile_anchor_offset_transfer_t2_kernel(
                 out=h1f[:, h, cols, :], in0=b[:].rearrange("m t c -> m c t"), in1=x_t[:, h, cols, :], op=ADD
             )
 
+        h1_tmp = {}
+
+        def s1_empty(h, ch, b):
+            t = sb("t_%d_%d" % (h, ch), [P, P, 4], F32, tag="s", bufs=2)
+            nc.scalar.copy(out=t[:], in_=b[:].rearrange("m t c -> m c t"))
+            h1_tmp[h, ch] = t
+
+        def s1_add_gp(h, ch):
+            cols = slice(P * ch, P * (ch + 1))
+            nc.gpsimd.tensor_tensor(out=h1f[:, h, cols, :], in0=h1_tmp[h, ch][:], in1=x_t[:, h, cols, :], op=ADD)
+
         h1b = {}
 
         def h1_round(h, ch):
             hc, cc = divmod(ch, 4)
-            if cc == 0:
-                h1b[h, hc] = sb("h1b%d%d" % (h, hc), [P, 512, 4], BF16, tag="h1b", bufs=2)
+            if (h, hc) not in h1b:
+                h1b[h, hc] = sb("h1b%d%d" % (h, hc), [P, 512, 4], BF16, tag="h1b", bufs=3)
             dst = h1b[h, hc][:].rearrange("m (u p e) t -> m u p (e t)", u=2, e=2)
             src = h1f[:, h, P * ch : P * (ch + 1), :].rearrange("m (p u e) t -> m u p (e t)", u=2, e=2)
-            nc.scalar.copy(out=dst[:, :, 32 * cc : 32 * cc + 32, :], in_=src)
+            dst = dst[:, :, 32 * cc : 32 * cc + 32, :]
+            if (h, ch) in G_RD:
+                nc.gpsimd.tensor_scalar(out=dst, in0=src, scalar1=1.0, scalar2=0.0, op0=MULT, op1=ADD)
+            else:
+                nc.scalar.copy(out=dst, in_=src)
 
         def h1_quant(h, hc):
             nc.vector.quantize_mx(
@@ -177,20 +215,16 @@ def tile_anchor_offset_transfer_t2_kernel(
                 in_=h1b[h, hc][:].rearrange("m c t -> m (c t)"),
             )
 
-        def h1_gain(a, hc):
-            for t in range(4):
-                v = h1f[:, a, 512 * hc : 512 * hc + 512, t].rearrange("m (p u e) -> m u p e", u=2, e=2)
-                nc.gpsimd.tensor_scalar(
-                    out=h1g[:, a, t, hc, :].rearrange("m (u p e) -> m u p e", u=2, e=2),
-                    in0=v,
-                    scalar1=gain_f[:, a, t : t + 1],
-                    scalar2=0.0,
-                    op0=MULT,
-                    op1=ADD,
+        def b_permute_gp(a, k, part):
+            m0 = 16 * part
+            for src, dst, w in ((b_raw, b_w, 2), (bs_raw, b_s, 1)):
+                nc.gpsimd.tensor_copy(
+                    out=dst[:, k, 512 * w * a : 512 * w * (a + 1)].rearrange("p (t m b) -> p t m b", t=4, b=w)[:, :, m0 : m0 + 16],
+                    in_=src[:, k, 512 * w * a : 512 * w * (a + 1)].rearrange("p (m t b) -> p t m b", t=4, b=w)[:, :, m0 : m0 + 16],
                 )
 
-        def b_permute(a):
-            for k in range(2):
+        def b_permute(a, k):
+            if True:
                 nc.vector.tensor_copy(
                     out=b_w[:, k, 1024 * a : 1024 * a + 1024].rearrange("p (t m b) -> p t m b", t=4, b=2),
                     in_=b_raw[:, k, 1024 * a : 1024 * a + 1024].rearrange("p (m t b) -> p t m b", t=4, b=2),
@@ -218,40 +252,50 @@ def tile_anchor_offset_transfer_t2_kernel(
                 )
             return b
 
+        z_tiles = {}
+
         def s2_add(a, hc, t, b):
-            if a not in h2t:
-                h2t[a] = sb("h2t%d" % a, [P, 4, 2, 512], BF16, tag="r2", bufs=2)
-            nc.vector.scalar_tensor_tensor(
-                out=h2t[a][:, t, hc, :],
-                in0=b[:],
-                scalar=gain_f[:, a, t : t + 1],
-                in1=h1g[:, a, t, hc, :],
-                op0=MULT,
-                op1=ADD,
+            z_tiles[a, hc, t] = sb("z_%d%d%d" % (a, hc, t), [P, 512], F32, tag="z", bufs=3)
+            nc.vector.tensor_tensor(
+                out=z_tiles[a, hc, t][:].rearrange("m (u p e) -> m u p e", u=2, e=2),
+                in0=b[:].rearrange("m (u p e) -> m u p e", u=2, e=2),
+                in1=h1f[:, a, 512 * hc : 512 * hc + 512, t].rearrange("m (p u e) -> m u p e", u=2, e=2),
+                op=ADD,
             )
 
-        def h2_transpose(a, hc):
-            words = h2t[a][:].rearrange("m t k c -> m (t k c)").bitcast(F32)
-            banks = []
-            for tp in range(2):
-                b = bank("ht%d%d%d" % (a, hc, tp), [P, 2, 2, P])
-                for tt in range(2):
-                    base = ((2 * tp + tt) * 2 + hc) * 256
-                    for u in range(2):
-                        nc.tensor.transpose(b[:, tt, u, :], words[:, base + P * u : base + P * (u + 1)], ident[:])
-                banks.append((tp, b))
-            return banks
+        def h2_gain(a, hc, t):
+            if a not in h2t:
+                h2t[a] = sb("h2t%d" % a, [P, 4, 2, 512], BF16, tag="r2", bufs=2)
+            if (a, hc, t) in G_HS:
+                nc.gpsimd.tensor_scalar(
+                    out=h2t[a][:, t, hc, :], in0=z_tiles[a, hc, t][:], scalar1=gain_f[:, a, t : t + 1], scalar2=0.0, op0=MULT, op1=ADD
+                )
+                return
+            nc.scalar.activation(
+                out=h2t[a][:, t, hc, :],
+                in_=z_tiles[a, hc, t][:],
+                func=mybir.ActivationFunctionType.Copy,
+                scale=gain_f[:, a, t : t + 1],
+            )
 
-        def h2_empty(a, hc, banks):
+        def h2_transpose(a, hc, tp):
+            words = h2t[a][:].rearrange("m t k c -> m (t k c)").bitcast(F32)
+            b = bank("ht%d%d%d" % (a, hc, tp), [P, 2, 2, P])
+            for tt in range(2):
+                base = ((2 * tp + tt) * 2 + hc) * 256
+                for u in range(2):
+                    nc.tensor.transpose(b[:, tt, u, :], words[:, base + P * u : base + P * (u + 1)], ident[:])
+            return b
+
+        def h2_empty(a, hc, tp, b):
             if a not in h2i:
                 h2i[a] = sb("h2i%d" % a, [P, 2, 512, 4], BF16, tag="r1", bufs=2)
             words = h2i[a][:].rearrange("p k g j -> p (k g j)").bitcast(F32)
-            for tp, b in banks:
-                base = (hc * 512 + tp * 256) * 2
-                nc.scalar.copy(
-                    out=words[:, base : base + 512].rearrange("p (t m u) -> p t m u", t=2, u=2),
-                    in_=b[:].rearrange("p t u m -> p t m u"),
-                )
+            base = (hc * 512 + tp * 256) * 2
+            nc.scalar.copy(
+                out=words[:, base : base + 512].rearrange("p (t m u) -> p t m u", t=2, u=2),
+                in_=b[:].rearrange("p t u m -> p t m u"),
+            )
 
         def h2_quant(a, hc):
             nc.vector.quantize_mx(
@@ -260,9 +304,10 @@ def tile_anchor_offset_transfer_t2_kernel(
                 in_=h2i[a][:, hc, :, :].rearrange("p g j -> p (g j)"),
             )
 
-        def s3_mm(a, i):
-            b = bank("s3_%d_%d" % (a, i), [P, 512])
-            for k in range(2):
+        def s3_mm(a, i, ks=(0, 1), b=None):
+            if b is None:
+                b = bank("s3_%d_%d" % (a, i), [P, 512])
+            for k in ks:
                 nc.tensor.matmul_mx(
                     out=b[:],
                     lhsT=e_w[:, k, 2 * P * i : 2 * P * (i + 1)].bitcast(FP4X4),
@@ -274,106 +319,189 @@ def tile_anchor_offset_transfer_t2_kernel(
                 )
             return b
 
-        def s3_add(a, i, b):
-            o = sb("o_%d_%d" % (a, i), [P, P, 4], F32, tag="o", bufs=6)
-            y_cols = y_sb[:, i, 512 * a : 512 * a + 512].rearrange("p (m t) -> p m t", t=4)
-            b_cols = b[:].rearrange("p (t m) -> p m t", t=4)
-            if (16 * a + i) % G_EVERY == G_EVERY - 1 and 16 * a + i < 30:
-                s = sb("s_%d_%d" % (a, i), [P, P, 4], F32, tag="s", bufs=2)
-                nc.scalar.copy(out=s[:], in_=b_cols)
-                nc.gpsimd.tensor_tensor(out=o[:], in0=s[:], in1=y_cols, op=ADD)
-                return (True, a, i, o)
-            nc.vector.tensor_tensor(out=o[:], in0=b_cols, in1=y_cols, op=ADD)
-            return (False, a, i, o)
+        o_tiles = {}
+        s_tiles = {}
 
-        def store(item):
-            slow, a, i, o = item
+        def y_cols(n):
+            a, i = divmod(n, 16)
+            return y_sb[:, i, 512 * a : 512 * a + 512].rearrange("p (m t) -> p m t", t=4)
+
+        def out_add(n, b):
+            o_tiles[n] = sb("o_%d" % n, [P, P, 4], F32, tag="o", bufs=O_BUFS)
+            nc.vector.tensor_tensor(out=o_tiles[n][:], in0=b[:].rearrange("p (t m) -> p m t", t=4), in1=y_cols(n), op=ADD)
+
+        def out_empty(n, b):
+            s_tiles[n] = sb("s_%d" % n, [P, P, 4], F32, tag="s", bufs=2)
+            nc.scalar.copy(out=s_tiles[n][:], in_=b[:].rearrange("p (t m) -> p m t", t=4))
+
+        def out_add_gp(n):
+            o_tiles[n] = sb("g_%d" % n, [P, P, 4], F32, tag="g", bufs=3)
+            nc.gpsimd.tensor_tensor(out=o_tiles[n][:], in0=s_tiles[n][:], in1=y_cols(n), op=ADD)
+
+        def store(n):
+            a, i = divmod(n, 16)
             nc.sync.dma_start(
-                out=out[P * i : P * (i + 1), 512 * a : 512 * a + 512], in_=o[:].rearrange("p m t -> p (m t)")
+                out=out[P * i : P * (i + 1), 512 * a : 512 * a + 512], in_=o_tiles[n][:].rearrange("p m t -> p (m t)")
             )
 
-        xi_scalar(0)
-        xi_vector(0)
-        tr = x_transpose(0)
-        x_quant(0)
-        x_empty(0, tr)
-        for ch in range(3):
-            s1_add(0, ch, s1_mm(0, ch))
-        b3 = s1_mm(0, 3)
-        xi_scalar(1)
-        xi_vector(1)
-        tr = x_transpose(1)
-        s1_add(0, 3, b3)
-        x_quant(1)
-        h1_round(0, 0)
-        x_empty(1, tr)
-        for ch in range(1, 4):
-            h1_round(0, ch)
-        h1_gain(0, 0)
-        for ch in range(4, 8):
-            s1_add(0, ch, s1_mm(0, ch))
-            h1_round(0, ch)
-            if ch == 5:
-                h1_quant(0, 0)
-        b_permute(0)
-        h1_gain(0, 1)
-        for ch in range(8):
-            s1_add(1, ch, s1_mm(1, ch))
-            h1_round(1, ch)
-            if ch == 0:
-                h1_quant(0, 1)
-            if ch == 3:
-                h1_gain(1, 0)
-            if ch == 4:
-                b_permute(1)
-            if ch == 5:
-                h1_quant(1, 0)
-        h1_gain(1, 1)
-        for t in range(4):
-            s2_add(0, 0, t, s2_mm(0, 0, t))
-            if t == 1:
-                h1_quant(1, 1)
-        b01 = [s2_mm(0, 1, t) for t in range(4)]
-        tr00 = h2_transpose(0, 0)
-        h2_empty(0, 0, tr00)
-        for t in range(4):
-            s2_add(0, 1, t, b01[t])
-        b10 = [s2_mm(1, 0, t) for t in range(2)]
-        tr01 = h2_transpose(0, 1)
-        b10 += [s2_mm(1, 0, t) for t in range(2, 4)]
-        h2_empty(0, 1, tr01)
-        h2_quant(0, 0)
-        s2_add(1, 0, 0, b10[0])
-        s2_add(1, 0, 1, b10[1])
-        h2_quant(0, 1)
-        s2_add(1, 0, 2, b10[2])
-        s2_add(1, 0, 3, b10[3])
-        b11 = [s2_mm(1, 1, t) for t in range(4)]
-        tr10 = h2_transpose(1, 0)
-        h2_empty(1, 0, tr10)
-        for t in range(4):
-            s2_add(1, 1, t, b11[t])
+        banks = {}
+        done = set()
+        live = [0]
+
+        def pe(name, needs, fn, *args):
+            def go():
+                banks[name] = fn(*args)
+                live[0] += 1
+            return (name, needs, go, True)
+
+        def use(name, needs, src, fn, *args):
+            def go():
+                fn(*(args + (banks[src],)))
+                live[0] -= 1
+            return (name, needs + [src], go, False)
+
+        def do(name, needs, fn, *args):
+            return (name, needs, lambda: fn(*args), False)
+
+        q_pe, q_v, q_s, q_g, q_d = [], [], [], [], []
+        H = range(2)
+        for h in H:
+            for k in H:
+                pass
+
+        def PE_tr(h):
+            return [pe(("tr", h, k, jp), [], x_transpose, h, k, jp) for k in H for jp in H]
+
+        def PE_s1(h, chs):
+            return [pe(("s1", h, ch), [("xq", h, 0), ("xq", h, 1)], s1_mm, h, ch) for ch in chs]
+
+        def PE_s2(a, hc, ts=range(4)):
+            return [pe(("s2", a, hc, t), [("q1", 0, hc), ("q1", 1, hc), ("bp", a, 0), ("bp", a, 1)], s2_mm, a, hc, t) for t in ts]
+
+        def PE_ht(a, hc):
+            return [pe(("ht", a, hc, tp), [("hs", a, hc, 2 * tp), ("hs", a, hc, 2 * tp + 1)], h2_transpose, a, hc, tp) for tp in H]
+
+        def PE_s3a(ns):
+            return [pe(("s3a", n), [("q2", n // 16, 0)], s3_mm, n // 16, n % 16, (0,)) for n in ns]
+
+        def PE_s3b(ns):
+            def fin(n):
+                banks[("s3", n)] = s3_mm(n // 16, n % 16, (1,), banks[("s3a", n)])
+
+            return [do(("s3", n), [("s3a", n), ("q2", n // 16, 1)], fin, n) for n in ns]
+
+        def PE_s3(ns):
+            return [pe(("s3", n), [("q2", n // 16, 0), ("q2", n // 16, 1)], s3_mm, n // 16, n % 16) for n in ns]
+
+        def V_x(h, k):
+            return [do(("xi", h, k), [], xi_vector, h, k), do(("xq", h, k), [("xi", h, k), ("xis", h, k)] + ([("xig", h, k)] if h == 1 and G_BLOCKS else []), x_quant, h, k)]
+
+        def V_tt(h, chs):
+            return [use(("tt", h, ch), [("xe", h, ch // 4, 0), ("xe", h, ch // 4, 1)], ("s1", h, ch), s1_add, h, ch) for ch in chs if (h, ch) not in G_ADD]
+
+        def S_a1(h, ch):
+            return [use(("sa", h, ch), [], ("s1", h, ch), s1_empty, h, ch)] if (h, ch) in G_ADD else []
+
+        def G_a1(h, ch):
+            return [do(("tt", h, ch), [("sa", h, ch), ("xe", h, ch // 4, 0), ("xe", h, ch // 4, 1)], s1_add_gp, h, ch)] if (h, ch) in G_ADD else []
+
+        def G_xi(h, k):
+            return [do(("xig", h, k), [], xi_gpsimd, h, k)] if G_BLOCKS else []
+
+
+        def V_q1(h, hc):
+            return [do(("q1", h, hc), [("rd", h, ch) for ch in range(4 * hc, 4 * hc + 4)], h1_quant, h, hc)]
+
+        def V_bp(a, k):
+            if (a, k) in G_BP:
+                return []
+            return [do(("bp", a, k), [], b_permute, a, k)]
+
+        def V_st(a, hc, ts=range(4)):
+            return [use(("st", a, hc, t), [("tt", a, ch) for ch in range(4 * hc, 4 * hc + 4)], ("s2", a, hc, t), s2_add, a, hc, t) for t in ts]
+
+        def V_q2(a, hc):
+            return [do(("q2", a, hc), [("he", a, hc, 0), ("he", a, hc, 1)], h2_quant, a, hc)]
+
+        def V_o(ns):
+            return [use(("o", n), [], ("s3", n), out_add, n) for n in ns if n not in G_OUT]
+
+        def G_bp(a, k):
+            return [do(("bpp", a, k, j) if j < 7 else ("bp", a, k), [], b_permute_gp, a, k, j) for j in range(8)] if (a, k) in G_BP else []
+
+        def S_xi(h, k):
+            return [do(("xis", h, k), [], xi_scalar, h, k)]
+
+        def S_xe(h, k):
+            return [use(("xe", h, k, jp), [], ("tr", h, k, jp), x_empty, h, k, jp) for jp in H]
+
+        def S_rd(h, chs):
+            return [do(("rd", h, ch), [("tt", h, ch)], h1_round, h, ch) for ch in chs]
+
+        def S_hs(a, hc, ts=range(4)):
+            return [do(("hs", a, hc, t), [("st", a, hc, t)], h2_gain, a, hc, t) for t in ts]
+
+        def S_he(a, hc):
+            return [use(("he", a, hc, tp), [], ("ht", a, hc, tp), h2_empty, a, hc, tp) for tp in H]
+
+        def S_o(ns):
+            return [use(("os", n), [("o", p) for p in G_OUT if p < n and sum(1 for z in G_OUT if p < z < n) >= 1], ("s3", n), out_empty, n) for n in ns if n in G_OUT]
+
+        def G_o(ns):
+            return [do(("o", n), [("os", n)], out_add_gp, n) for n in ns if n in G_OUT]
+
+        q_pe += PE_tr(0) + PE_s1(0, range(4)) + PE_tr(1) + PE_s1(0, range(4, 8)) + PE_s1(1, range(8))
+        q_pe += PE_s2(0, 0) + PE_s2(0, 1) + PE_ht(0, 0) + PE_ht(0, 1) + PE_s2(1, 0, (0, 1))
+        q_pe += PE_s3((0, 1)) + PE_s2(1, 0, (2,)) + PE_s3((2, 3)) + PE_s2(1, 0, (3,)) + PE_s3((4, 5)) + PE_s2(1, 1, (0,)) + PE_s3((6,))
+        q_pe += PE_ht(1, 0) + PE_s2(1, 1, (1,)) + PE_s3((7, 8)) + PE_s2(1, 1, (2,)) + PE_s3((9, 10)) + PE_s2(1, 1, (3,)) + PE_s3((11, 12, 13)) + PE_ht(1, 1) + PE_s3(range(14, 32))
+
+        q_v += V_x(0, 0) + V_x(0, 1) + V_tt(0, range(3)) + V_x(1, 0) + V_x(1, 1) + V_tt(0, range(3, 8))
+        q_v += V_bp(0, 0) + V_bp(0, 1) + V_tt(1, (0, 1, 2, 3)) + V_q1(0, 0) + V_q1(0, 1) + V_tt(1, (4, 5)) + V_q1(1, 0)
+        q_v += V_tt(1, (6, 7))
+        q_v += V_st(0, 0, (0, 1)) + V_q1(1, 1) + V_st(0, 0, (2, 3)) + V_st(0, 1) + V_bp(1, 0) + V_q2(0, 0) + V_bp(1, 1) + V_q2(0, 1)
+        q_v += V_st(1, 0, (0, 1)) + V_o((0, 1)) + V_st(1, 0, (2,)) + V_o((2, 3)) + V_st(1, 0, (3,)) + V_o((4, 5)) + V_st(1, 1, (0,)) + V_o((6,))
+        q_v += V_st(1, 1, (1,)) + V_o((7,)) + V_q2(1, 0) + V_o((8,)) + V_st(1, 1, (2,)) + V_o((9, 10)) + V_st(1, 1, (3,)) + V_o((11, 12, 13)) + V_q2(1, 1) + V_o(range(14, 32))
+
+        def HS(a, hc, ts=range(4)):
+            return S_hs(a, hc, [t for t in ts if (a, hc, t) not in G_HS])
+
+        q_s += S_xi(0, 0) + S_xi(0, 1) + S_xe(0, 0) + S_xe(0, 1) + S_xi(1, 0) + S_xi(1, 1)
+        seq = [(0, n) for n in range(8)] + [(1, n) for n in range(8)]
         late = []
-
-        def out_step(n, b):
-            a, i = divmod(n, 16)
-            item = s3_add(a, i, b)
-            if item[0]:
-                late.append((n, item))
+        for j, (h, ch) in enumerate(seq):
+            if (h, ch) in G_RD:
+                pass
+            elif (h, ch) in G_ADD:
+                late = S_rd(h, (ch,))
             else:
-                store(item)
-            while late and n - late[0][0] >= 3:
-                store(late.pop(0)[1])
+                q_s += S_rd(h, (ch,)) + late
+                late = []
+            if (h, ch) == (0, XE_AT):
+                q_s += S_xe(1, 0) + S_xe(1, 1)
+            if j + 2 < 16:
+                q_s += S_a1(*seq[j + 2])
+        q_s += late
+        q_s += HS(0, 0) + HS(0, 1, (0, 1)) + S_he(0, 0) + HS(0, 1, (2, 3)) + S_he(0, 1) + HS(1, 0, (0, 1)) + S_o((0, 1, 2)) + HS(1, 0, (2,)) + S_o((3, 4)) + HS(1, 0, (3,)) + S_o((5,)) + S_he(1, 0) + S_o((6,))
+        q_s += HS(1, 1, (0, 1)) + S_o((7, 8, 9)) + HS(1, 1, (2, 3)) + S_o((10, 11)) + S_he(1, 1) + S_o(range(12, 32))
+        q_g += G_xi(1, 0) + G_xi(1, 1)
+        for h in H:
+            for n in range(8):
+                q_g += G_a1(h, n) + (S_rd(h, (n,)) if (h, n) in G_RD else [])
+        for a in H:
+            for hc in H:
+                for t in range(4):
+                    q_g += S_hs(a, hc, (t,)) if (a, hc, t) in G_HS else []
+        q_g += G_o(range(32))
+        order = sorted(range(32), key=lambda n: n + (G_LAG if n in G_OUT else 0))
+        q_d += [do(("w", n), [("o", n)], store, n) for n in order]
 
-        s3 = {}
-        for n in range(2):
-            s3[n] = s3_mm(0, n)
-        tr11 = h2_transpose(1, 1)
-        h2_empty(1, 1, tr11)
-        h2_quant(1, 0)
-        for n in range(32):
-            if n not in s3:
-                s3[n] = s3_mm(n // 16, n % 16)
-            out_step(n, s3[n])
-            if n == 1:
-                h2_quant(1, 1)
+        queues = [q_pe, q_v, q_s, q_g, q_d]
+        while any(queues):
+            moved = False
+            for q in queues:
+                while q and all(n in done for n in q[0][1]) and not (q[0][3] and live[0] >= 8):
+                    name, needs, go, isbank = q.pop(0)
+                    go()
+                    done.add(name)
+                    moved = True
+            assert moved, [q[0][:2] for q in queues if q]

@@ -17,16 +17,16 @@ ADD = mybir.AluOpType.add
 MULT = mybir.AluOpType.mult
 
 P = 128
-V_BLOCKS = ((2, 3), (1, 1))
-G_BLOCKS = 0
+V_BLOCKS = ((2, 3), (0, 0))
+G_BLOCKS = 2
 G_RD = ()
-G_HS = ()
+G_HS = ((0, 0, 2), (0, 1, 1))
 G_BP = ()
 G_ADD = ()
-G_OUT = ()
+G_OUT = (1, 4, 7, 10, 13, 16)
 LOADS = ('x00', 'x01', 'g', 'as', 'aw', 'x10', 'x11', 'bw', 'bs')
 O_BUFS = 8
-G_LAG = 2.5
+G_LAG = 1.5
 XE_AT = 0
 
 
@@ -56,7 +56,7 @@ def tile_anchor_offset_transfer_t2_kernel(
         xq = sb("xq", [P, 2, G], U32)
         xs = sb("xs", [P, 2, G], U8)
         x_t = sb("x_t", [P, 2, C, 4], BF16)
-        h1f = sb("h1f", [P, 2, C, 4], F32)
+        h1f = sb("h1f", [P, 2, C // 2, 4, 2], F32)
         h1q = sb("h1q", [P, 2, C], U32)
         h1s = sb("h1s", [P, 2, C], U8)
         h2q = sb("h2q", [P, 2, G], U32)
@@ -89,6 +89,10 @@ def tile_anchor_offset_transfer_t2_kernel(
         def load_x_half(h, k):
             nc.sync.dma_start(out=x_raw[h][:, k, :, :], in_=x_v[k][:, :, 512 * h : 512 * h + 512])
 
+        def load_b_half(a):
+            src = b_words.rearrange("k p n -> p k n")[:, :, 1024 * a : 1024 * a + 1024]
+            nc.sync.dma_start(out=b_raw[:, :, 1024 * a : 1024 * a + 1024].bitcast(I32), in_=src.bitcast(I32))
+
         def load_gain():
             nc.sync.dma_start(out=gain_b[:], in_=gain.rearrange("(a m t) -> m a t", m=P, t=4))
             nc.gpsimd.tensor_copy(out=gain_f[:], in_=gain_b[:])
@@ -103,6 +107,8 @@ def tile_anchor_offset_transfer_t2_kernel(
             "aw": lambda: load_words(a_w, a_words),
             "bs": lambda: load_scales(bs_raw, b_scales),
             "bw": lambda: load_words(b_raw, b_words),
+            "bw0": lambda: load_b_half(0),
+            "bw1": lambda: load_b_half(1),
         }
         for step in LOADS:
             loads[step]()
@@ -180,7 +186,10 @@ def tile_anchor_offset_transfer_t2_kernel(
         def s1_add(h, ch, b):
             cols = slice(P * ch, P * (ch + 1))
             nc.vector.tensor_tensor(
-                out=h1f[:, h, cols, :], in0=b[:].rearrange("m t c -> m c t"), in1=x_t[:, h, cols, :], op=ADD
+                out=h1f[:, h, 64 * ch : 64 * ch + 64, :, :],
+                in0=b[:].rearrange("m t (c e) -> m c t e", e=2),
+                in1=x_t[:, h, cols, :].rearrange("m (c e) t -> m c t e", e=2),
+                op=ADD,
             )
 
         h1_tmp = {}
@@ -200,9 +209,8 @@ def tile_anchor_offset_transfer_t2_kernel(
             hc, cc = divmod(ch, 4)
             if (h, hc) not in h1b:
                 h1b[h, hc] = sb("h1b%d%d" % (h, hc), [P, 512, 4], BF16, tag="h1b", bufs=3)
-            dst = h1b[h, hc][:].rearrange("m (u p e) t -> m u p (e t)", u=2, e=2)
-            src = h1f[:, h, P * ch : P * (ch + 1), :].rearrange("m (p u e) t -> m u p (e t)", u=2, e=2)
-            dst = dst[:, :, 32 * cc : 32 * cc + 32, :]
+            dst = h1b[h, hc][:, P * cc : P * (cc + 1), :].rearrange("m (c e) t -> m c e t", e=2)
+            src = h1f[:, h, 64 * ch : 64 * ch + 64, :, :].rearrange("m c t e -> m c e t")
             if (h, ch) in G_RD:
                 nc.gpsimd.tensor_scalar(out=dst, in0=src, scalar1=1.0, scalar2=0.0, op0=MULT, op1=ADD)
             else:
@@ -257,9 +265,9 @@ def tile_anchor_offset_transfer_t2_kernel(
         def s2_add(a, hc, t, b):
             z_tiles[a, hc, t] = sb("z_%d%d%d" % (a, hc, t), [P, 512], F32, tag="z", bufs=3)
             nc.vector.tensor_tensor(
-                out=z_tiles[a, hc, t][:].rearrange("m (u p e) -> m u p e", u=2, e=2),
-                in0=b[:].rearrange("m (u p e) -> m u p e", u=2, e=2),
-                in1=h1f[:, a, 512 * hc : 512 * hc + 512, t].rearrange("m (p u e) -> m u p e", u=2, e=2),
+                out=z_tiles[a, hc, t][:].rearrange("m (c e) -> m c e", e=2),
+                in0=b[:].rearrange("m (c e) -> m c e", e=2),
+                in1=h1f[:, a, 256 * hc : 256 * hc + 256, t, :],
                 op=ADD,
             )
 
@@ -268,12 +276,14 @@ def tile_anchor_offset_transfer_t2_kernel(
                 h2t[a] = sb("h2t%d" % a, [P, 4, 2, 512], BF16, tag="r2", bufs=2)
             if (a, hc, t) in G_HS:
                 nc.gpsimd.tensor_scalar(
-                    out=h2t[a][:, t, hc, :], in0=z_tiles[a, hc, t][:], scalar1=gain_f[:, a, t : t + 1], scalar2=0.0, op0=MULT, op1=ADD
+                    out=h2t[a][:, t, hc, :].rearrange("m (u p e) -> m u p e", u=2, e=2),
+                    in0=z_tiles[a, hc, t][:].rearrange("m (p u e) -> m u p e", u=2, e=2),
+                    scalar1=gain_f[:, a, t : t + 1], scalar2=0.0, op0=MULT, op1=ADD
                 )
                 return
             nc.scalar.activation(
-                out=h2t[a][:, t, hc, :],
-                in_=z_tiles[a, hc, t][:],
+                out=h2t[a][:, t, hc, :].rearrange("m (u p e) -> m u p e", u=2, e=2),
+                in_=z_tiles[a, hc, t][:].rearrange("m (p u e) -> m u p e", u=2, e=2),
                 func=mybir.ActivationFunctionType.Copy,
                 scale=gain_f[:, a, t : t + 1],
             )
@@ -451,16 +461,18 @@ def tile_anchor_offset_transfer_t2_kernel(
             return [do(("o", n), [("os", n)], out_add_gp, n) for n in ns if n in G_OUT]
 
         q_pe += PE_tr(0) + PE_s1(0, range(4)) + PE_tr(1) + PE_s1(0, range(4, 8)) + PE_s1(1, range(8))
-        q_pe += PE_s2(0, 0) + PE_s2(0, 1) + PE_ht(0, 0) + PE_ht(0, 1) + PE_s2(1, 0, (0, 1))
-        q_pe += PE_s3((0, 1)) + PE_s2(1, 0, (2,)) + PE_s3((2, 3)) + PE_s2(1, 0, (3,)) + PE_s3((4, 5)) + PE_s2(1, 1, (0,)) + PE_s3((6,))
-        q_pe += PE_ht(1, 0) + PE_s2(1, 1, (1,)) + PE_s3((7, 8)) + PE_s2(1, 1, (2,)) + PE_s3((9, 10)) + PE_s2(1, 1, (3,)) + PE_s3((11, 12, 13)) + PE_ht(1, 1) + PE_s3(range(14, 32))
+        q_pe += PE_s2(0, 0) + PE_s2(0, 1) + PE_ht(0, 0) + PE_ht(0, 1) + PE_s3a(range(6))
+        q_pe += PE_s3b((0, 1)) + PE_s2(1, 0, (0,)) + PE_s3b((2,)) + PE_s2(1, 0, (1,)) + PE_s3b((3,)) + PE_s2(1, 0, (2,)) + PE_s3b((4,)) + PE_s2(1, 0, (3,))
+        q_pe += PE_s3b((5,)) + PE_s2(1, 1, (0,)) + PE_s3((6,)) + PE_ht(1, 0) + PE_s2(1, 1, (1,)) + PE_s3((7, 8)) + PE_s2(1, 1, (2,)) + PE_s3((9,))
+        q_pe += PE_s2(1, 1, (3,)) + PE_s3((10, 11, 12)) + PE_ht(1, 1) + PE_s3(range(13, 32))
 
-        q_v += V_x(0, 0) + V_x(0, 1) + V_tt(0, range(3)) + V_x(1, 0) + V_x(1, 1) + V_tt(0, range(3, 8))
-        q_v += V_bp(0, 0) + V_bp(0, 1) + V_tt(1, (0, 1, 2, 3)) + V_q1(0, 0) + V_q1(0, 1) + V_tt(1, (4, 5)) + V_q1(1, 0)
+        q_v += V_x(0, 0) + V_x(0, 1) + V_tt(0, range(3)) + V_x(1, 0) + V_x(1, 1) + V_tt(0, range(3, 4)) + V_bp(0, 0) + V_tt(0, range(4, 6)) + V_bp(0, 1) + V_tt(0, range(6, 8))
+        q_v += V_tt(1, (0, 1, 2, 3)) + V_q1(0, 0) + V_q1(0, 1) + V_tt(1, (4, 5)) + V_q1(1, 0)
         q_v += V_tt(1, (6, 7))
-        q_v += V_st(0, 0, (0, 1)) + V_q1(1, 1) + V_st(0, 0, (2, 3)) + V_st(0, 1) + V_bp(1, 0) + V_q2(0, 0) + V_bp(1, 1) + V_q2(0, 1)
-        q_v += V_st(1, 0, (0, 1)) + V_o((0, 1)) + V_st(1, 0, (2,)) + V_o((2, 3)) + V_st(1, 0, (3,)) + V_o((4, 5)) + V_st(1, 1, (0,)) + V_o((6,))
-        q_v += V_st(1, 1, (1,)) + V_o((7,)) + V_q2(1, 0) + V_o((8,)) + V_st(1, 1, (2,)) + V_o((9, 10)) + V_st(1, 1, (3,)) + V_o((11, 12, 13)) + V_q2(1, 1) + V_o(range(14, 32))
+        q_v += V_st(0, 0, (0, 1)) + V_q1(1, 1) + V_st(0, 0, (2, 3)) + V_st(0, 1) + V_q2(0, 0) + V_bp(1, 0) + V_q2(0, 1) + V_bp(1, 1)
+        q_v += V_o((0, 1)) + V_st(1, 0, (0,)) + V_o((2,)) + V_st(1, 0, (1,)) + V_o((3,)) + V_st(1, 0, (2,)) + V_o((4,)) + V_st(1, 0, (3,)) + V_o((5,))
+        q_v += V_st(1, 1, (0,)) + V_o((6,)) + V_st(1, 1, (1,)) + V_o((7,)) + V_q2(1, 0) + V_o((8,)) + V_st(1, 1, (2,)) + V_o((9,)) + V_st(1, 1, (3,))
+        q_v += V_o((10, 11, 12)) + V_q2(1, 1) + V_o(range(13, 32))
 
         def HS(a, hc, ts=range(4)):
             return S_hs(a, hc, [t for t in ts if (a, hc, t) not in G_HS])
@@ -481,7 +493,7 @@ def tile_anchor_offset_transfer_t2_kernel(
             if j + 2 < 16:
                 q_s += S_a1(*seq[j + 2])
         q_s += late
-        q_s += HS(0, 0) + HS(0, 1, (0, 1)) + S_he(0, 0) + HS(0, 1, (2, 3)) + S_he(0, 1) + HS(1, 0, (0, 1)) + S_o((0, 1, 2)) + HS(1, 0, (2,)) + S_o((3, 4)) + HS(1, 0, (3,)) + S_o((5,)) + S_he(1, 0) + S_o((6,))
+        q_s += HS(0, 0) + HS(0, 1, (0, 1)) + S_he(0, 0) + HS(0, 1, (2, 3)) + S_he(0, 1) + S_o(range(0, 3)) + HS(1, 0, (0, 1)) + S_o((3, 4)) + HS(1, 0, (2,)) + HS(1, 0, (3,)) + S_o((5,)) + S_he(1, 0) + S_o((6,))
         q_s += HS(1, 1, (0, 1)) + S_o((7, 8, 9)) + HS(1, 1, (2, 3)) + S_o((10, 11)) + S_he(1, 1) + S_o(range(12, 32))
         q_g += G_xi(1, 0) + G_xi(1, 1)
         for h in H:

@@ -20,11 +20,11 @@ P = 128
 V_BLOCKS = ((2, 3), (0, 0))
 G_BLOCKS = 2
 G_RD = ()
-G_HS = ((0, 0, 2), (0, 1, 1))
+G_HS = ((0, 0, 1), (0, 0, 3), (0, 1, 1), (0, 1, 2))
 G_BP = ()
 G_ADD = ()
-G_OUT = (1, 4, 7, 10, 13, 16)
-LOADS = ('x00', 'x01', 'g', 'as', 'aw', 'x10', 'x11', 'bw', 'bs')
+G_OUT = (1, 4, 7, 10, 13, 16, 19, 22, 25, 28)
+LOADS = ('x00', 'x01', 'a0', 'g', 'as', 'aw', 'x10', 'x11', 'bw', 'bs')
 O_BUFS = 8
 G_LAG = 1.5
 XE_AT = 0
@@ -51,6 +51,7 @@ def tile_anchor_offset_transfer_t2_kernel(
         bs_raw = sb("bs_raw", [P, 2, G], U8)
         b_w = sb("b_w", [P, 2, 2 * G], U8)
         b_s = sb("b_s", [P, 2, G], U8)
+        a_0 = sb("a_0", [P, 2 * P], U8)
         e_w = sb("e_w", [P, 2, 2 * D], U8)
         e_s = sb("e_s", [P, 2, D], U8)
         xq = sb("xq", [P, 2, G], U32)
@@ -102,6 +103,7 @@ def tile_anchor_offset_transfer_t2_kernel(
             "x01": lambda: load_x_half(0, 1),
             "x10": lambda: load_x_half(1, 0),
             "x11": lambda: load_x_half(1, 1),
+            "a0": lambda: nc.sync.dma_start(out=a_0[:].bitcast(I32), in_=a_words[0][:, 0 : 2 * P].bitcast(I32)),
             "g": load_gain,
             "as": lambda: load_scales(a_s, a_scales),
             "aw": lambda: load_words(a_w, a_words),
@@ -167,6 +169,19 @@ def tile_anchor_offset_transfer_t2_kernel(
             dst = words[:, base : base + 1024].rearrange("m (p j u) -> m p j u", j=4, u=2)
             nc.scalar.copy(out=dst[:, :, 2 * jp : 2 * jp + 2, :], in_=b[:].rearrange("m j u p -> m p j u"))
 
+        def keep_busy(name, n, words, scales, k, cols):
+            b = bank(name, [P, 512])
+            for i in range(n):
+                nc.tensor.matmul_mx(
+                    out=b[:],
+                    lhsT=a_0[:].bitcast(FP4X4),
+                    lhsT_scale=a_s[:, 0, 0:P],
+                    rhs=words[:, k, cols : cols + 512].bitcast(FP8X4),
+                    rhs_scale=scales[:, k, cols : cols + 512],
+                    start=True,
+                    stop=True,
+                )
+
         def s1_mm(h, ch):
             b = bank("s1_%d_%d" % (h, ch), [P, 4, P])
             for t in range(4):
@@ -206,21 +221,20 @@ def tile_anchor_offset_transfer_t2_kernel(
         h1b = {}
 
         def h1_round(h, ch):
-            hc, cc = divmod(ch, 4)
-            if (h, hc) not in h1b:
-                h1b[h, hc] = sb("h1b%d%d" % (h, hc), [P, 512, 4], BF16, tag="h1b", bufs=3)
-            dst = h1b[h, hc][:, P * cc : P * (cc + 1), :].rearrange("m (c e) t -> m c e t", e=2)
+            if h not in h1b:
+                h1b[h] = sb("h1b%d" % h, [P, C, 4], BF16)
+            dst = h1b[h][:, P * ch : P * (ch + 1), :].rearrange("m (c e) t -> m c e t", e=2)
             src = h1f[:, h, 64 * ch : 64 * ch + 64, :, :].rearrange("m c t e -> m c e t")
             if (h, ch) in G_RD:
                 nc.gpsimd.tensor_scalar(out=dst, in0=src, scalar1=1.0, scalar2=0.0, op0=MULT, op1=ADD)
             else:
                 nc.scalar.copy(out=dst, in_=src)
 
-        def h1_quant(h, hc):
+        def h1_quant(h, c0, n):
             nc.vector.quantize_mx(
-                out=h1q[:, h, 512 * hc : 512 * hc + 512].bitcast(FP8X4),
-                scales=h1s[:, h, 512 * hc : 512 * hc + 512],
-                in_=h1b[h, hc][:].rearrange("m c t -> m (c t)"),
+                out=h1q[:, h, c0 : c0 + n].bitcast(FP8X4),
+                scales=h1s[:, h, c0 : c0 + n],
+                in_=h1b[h][:, c0 : c0 + n, :].rearrange("m c t -> m (c t)"),
             )
 
         def b_permute_gp(a, k, part):
@@ -231,15 +245,16 @@ def tile_anchor_offset_transfer_t2_kernel(
                     in_=src[:, k, 512 * w * a : 512 * w * (a + 1)].rearrange("p (m t b) -> p t m b", t=4, b=w)[:, :, m0 : m0 + 16],
                 )
 
-        def b_permute(a, k):
-            if True:
+        def b_permute(a, part):
+            if part == 0:
                 nc.vector.tensor_copy(
-                    out=b_w[:, k, 1024 * a : 1024 * a + 1024].rearrange("p (t m b) -> p t m b", t=4, b=2),
-                    in_=b_raw[:, k, 1024 * a : 1024 * a + 1024].rearrange("p (m t b) -> p t m b", t=4, b=2),
+                    out=b_w[:, :, 1024 * a : 1024 * a + 1024].rearrange("p k (t m b) -> p k t m b", t=4, b=2),
+                    in_=b_raw[:, :, 1024 * a : 1024 * a + 1024].rearrange("p k (m t b) -> p k t m b", t=4, b=2),
                 )
+            else:
                 nc.vector.tensor_copy(
-                    out=b_s[:, k, 512 * a : 512 * a + 512].rearrange("p (t m) -> p t m", t=4),
-                    in_=bs_raw[:, k, 512 * a : 512 * a + 512].rearrange("p (m t) -> p t m", t=4),
+                    out=b_s[:, :, 512 * a : 512 * a + 512].rearrange("p k (t m) -> p k t m", t=4),
+                    in_=bs_raw[:, :, 512 * a : 512 * a + 512].rearrange("p k (m t) -> p k t m", t=4),
                 )
 
         h2t = {}
@@ -420,7 +435,14 @@ def tile_anchor_offset_transfer_t2_kernel(
 
 
         def V_q1(h, hc):
-            return [do(("q1", h, hc), [("rd", h, ch) for ch in range(4 * hc, 4 * hc + 4)], h1_quant, h, hc)]
+            if h == 0:
+                if hc == 0:
+                    return []
+                return [
+                    do(("q1", 0, 1), [("rd", h, ch) for ch in range(8)], h1_quant, 0, 0, C),
+                    do(("q1", 0, 0), [("q1", 0, 1)], lambda: None),
+                ]
+            return [do(("q1", h, hc), [("rd", h, ch) for ch in range(4 * hc, 4 * hc + 4)], h1_quant, h, 512 * hc, 512)]
 
         def V_bp(a, k):
             if (a, k) in G_BP:
@@ -460,13 +482,22 @@ def tile_anchor_offset_transfer_t2_kernel(
         def G_o(ns):
             return [do(("o", n), [("os", n)], out_add_gp, n) for n in ns if n in G_OUT]
 
-        q_pe += PE_tr(0) + PE_s1(0, range(4)) + PE_tr(1) + PE_s1(0, range(4, 8)) + PE_s1(1, range(8))
-        q_pe += PE_s2(0, 0) + PE_s2(0, 1) + PE_ht(0, 0) + PE_ht(0, 1) + PE_s3a(range(6))
+        def W1(n):
+            return [do(("w1",), [("xq", 0, 0)], keep_busy, "w1", n, xq, xs, 0, 0)]
+
+        def W2(n):
+            return [do(("w2",), [("xq", 1, 0)], keep_busy, "w2", n, xq, xs, 1, 0)]
+
+        def W3(n):
+            return [do(("w3",), [("q1", 1, 0)], keep_busy, "w3", n, h1q, h1s, 1, 0)]
+
+        q_pe += PE_tr(0) + W1(3) + PE_s1(0, range(4)) + PE_tr(1) + PE_s1(0, range(4, 8)) + PE_s1(1, range(8))
+        q_pe += W2(4) + PE_s2(0, 0) + PE_s2(0, 1) + PE_ht(0, 0) + W3(3) + PE_ht(0, 1) + PE_s3a(range(6))
         q_pe += PE_s3b((0, 1)) + PE_s2(1, 0, (0,)) + PE_s3b((2,)) + PE_s2(1, 0, (1,)) + PE_s3b((3,)) + PE_s2(1, 0, (2,)) + PE_s3b((4,)) + PE_s2(1, 0, (3,))
         q_pe += PE_s3b((5,)) + PE_s2(1, 1, (0,)) + PE_s3((6,)) + PE_ht(1, 0) + PE_s2(1, 1, (1,)) + PE_s3((7, 8)) + PE_s2(1, 1, (2,)) + PE_s3((9,))
         q_pe += PE_s2(1, 1, (3,)) + PE_s3((10, 11, 12)) + PE_ht(1, 1) + PE_s3(range(13, 32))
 
-        q_v += V_x(0, 0) + V_x(0, 1) + V_tt(0, range(3)) + V_x(1, 0) + V_x(1, 1) + V_tt(0, range(3, 4)) + V_bp(0, 0) + V_tt(0, range(4, 6)) + V_bp(0, 1) + V_tt(0, range(6, 8))
+        q_v += V_x(0, 0) + V_x(0, 1) + V_tt(0, range(3)) + V_x(1, 0) + V_tt(0, range(3, 4)) + V_x(1, 1) + V_bp(0, 0) + V_tt(0, range(4, 6)) + V_bp(0, 1) + V_tt(0, range(6, 8))
         q_v += V_tt(1, (0, 1, 2, 3)) + V_q1(0, 0) + V_q1(0, 1) + V_tt(1, (4, 5)) + V_q1(1, 0)
         q_v += V_tt(1, (6, 7))
         q_v += V_st(0, 0, (0, 1)) + V_q1(1, 1) + V_st(0, 0, (2, 3)) + V_st(0, 1) + V_q2(0, 0) + V_bp(1, 0) + V_q2(0, 1) + V_bp(1, 1)

from contextlib import ExitStack

import concourse.mybir as mybir
from concourse.masks import make_identity

C, G, D = 1024, 1024, 2048
FLOPS = 2 * C * C * G + 2 * C * G * G + 2 * C * D * G

F32 = mybir.dt.float32
BF16 = mybir.dt.bfloat16
I32 = mybir.dt.int32
U32 = mybir.dt.uint32
U8 = mybir.dt.uint8
FP8X4 = mybir.dt.float8_e4m3fn_x4
FP4X4 = mybir.dt.float4_e2m1fn_x4
ADD = mybir.AluOpType.add
MULT = mybir.AluOpType.mult

P = 128
V_BLOCKS = ((2, 3), (0, 0))
G_BLOCKS = 2
G_RD = ()
G_HS = ((0, 0, 1), (0, 0, 3), (0, 1, 1), (0, 1, 2))
G_BP = ()
G_ADD = ()
G_OUT = (1, 4, 7, 10, 13, 16, 19, 22, 25, 28)
LOADS = ('x00', 'x01', 'a0', 'g', 'as', 'aw', 'x10', 'x11', 'bw', 'bs')
O_BUFS = 8
G_LAG = 1.5
XE_AT = 0


def tile_anchor_offset_transfer_t2_kernel(
    tc, x, a_words, a_scales, b_words, b_scales, gain, e_words, e_scales, y, out
):
    nc = tc.nc
    with ExitStack() as ctx:
        keep = ctx.enter_context(tc.tile_pool(name="keep", bufs=1))
        psum = ctx.enter_context(tc.psum_pool(name="psum", bufs=8))
        ctx.enter_context(tc.manual_schedule())

        def sb(name, shape, dtype, tag=None, bufs=1):
            return keep.tile(shape, dtype, name=name, tag=tag or name, bufs=bufs, align_bytes=256)

        def bank(name, shape):
            return psum.tile(shape, F32, name=name, tag="bank", bufs=8)

        a_w = sb("a_w", [P, 2, 2 * C], U8)
        a_s = sb("a_s", [P, 2, C], U8)
        b_raw = sb("b_raw", [P, 2, 2 * G], U8)
        bs_raw = sb("bs_raw", [P, 2, G], U8)
        b_w = sb("b_w", [P, 2, 2 * G], U8)
        b_s = sb("b_s", [P, 2, G], U8)
        a_0 = sb("a_0", [P, 2 * P], U8)
        e_w = sb("e_w", [P, 2, 2 * D], U8)
        e_s = sb("e_s", [P, 2, D], U8)
        xq = sb("xq", [P, 2, G], U32)
        xs = sb("xs", [P, 2, G], U8)
        x_t = sb("x_t", [P, 2, C, 4], BF16)
        h1f = sb("h1f", [P, 2, C // 2, 4, 2], F32)
        h1q = sb("h1q", [P, 2, C], U32)
        h1s = sb("h1s", [P, 2, C], U8)
        h2q = sb("h2q", [P, 2, G], U32)
        h2s = sb("h2s", [P, 2, G], U8)
        y_sb = sb("y_sb", [P, D // P, G], BF16)
        gain_b = sb("gain_b", [P, 2, 4], BF16)
        gain_f = sb("gain_f", [P, 2, 4], F32)
        ident = sb("ident", [P, P], F32)
        warm = sb("warm", [P, 8], F32)
        x_raw = [sb("x_raw%d" % h, [P, 2, 4, 512], BF16, tag="r1", bufs=2) for h in range(2)]
        xi = [sb("xi%d" % h, [P, 2, 4, P, 4], BF16, tag="r2", bufs=2) for h in range(2)]

        nc.vector.memset(a_s[:].bitcast(I32), 0)
        nc.vector.memset(warm[:], 0.0)
        nc.vector.memset(bs_raw[:].bitcast(I32), 0)
        nc.vector.memset(e_s[:].bitcast(I32), 0)
        nc.scalar.copy(out=warm[:, 4:5], in_=warm[:, 0:1])
        make_identity(nc, ident[:])

        x_v = x.rearrange("(k p j) w -> k p j w", k=2, p=P)

        def load_scales(dst, src):
            s_v = src.rearrange("k (q r) n -> r q k n", r=4)
            for r in range(4):
                nc.sync.dma_start(out=dst[r:P:32, :, :].bitcast(I32), in_=s_v[r].bitcast(I32))

        def load_words(dst, src):
            nc.sync.dma_start(out=dst[:].bitcast(I32), in_=src.rearrange("k p n -> p k n").bitcast(I32))

        def load_x_half(h, k):
            nc.sync.dma_start(out=x_raw[h][:, k, :, :], in_=x_v[k][:, :, 512 * h : 512 * h + 512])

        def load_b_half(a):
            src = b_words.rearrange("k p n -> p k n")[:, :, 1024 * a : 1024 * a + 1024]
            nc.sync.dma_start(out=b_raw[:, :, 1024 * a : 1024 * a + 1024].bitcast(I32), in_=src.bitcast(I32))

        def load_gain():
            nc.sync.dma_start(out=gain_b[:], in_=gain.rearrange("(a m t) -> m a t", m=P, t=4))
            nc.gpsimd.tensor_copy(out=gain_f[:], in_=gain_b[:])

        loads = {
            "x00": lambda: load_x_half(0, 0),
            "x01": lambda: load_x_half(0, 1),
            "x10": lambda: load_x_half(1, 0),
            "x11": lambda: load_x_half(1, 1),
            "a0": lambda: nc.sync.dma_start(out=a_0[:].bitcast(I32), in_=a_words[0][:, 0 : 2 * P].bitcast(I32)),
            "g": load_gain,
            "as": lambda: load_scales(a_s, a_scales),
            "aw": lambda: load_words(a_w, a_words),
            "bs": lambda: load_scales(bs_raw, b_scales),
            "bw": lambda: load_words(b_raw, b_words),
            "bw0": lambda: load_b_half(0),
            "bw1": lambda: load_b_half(1),
        }
        for step in LOADS:
            loads[step]()
        load_words(e_w, e_words)
        load_scales(e_s, e_scales)
        y_v = y.rearrange("(i p) g -> p i g", p=P)
        for i in range(0, D // P, 4):
            nc.sync.dma_start(out=y_sb[:, i : i + 4, :], in_=y_v[:, i : i + 4, :])

        def xi_block(h, k, t0, n, engine_copy):
            v = x_raw[h][:, k, :, :].rearrange("p j (m t) -> p t m j", t=4)
            engine_copy(out=xi[h][:, k, t0 : t0 + n, :, :], in_=v[:, t0 : t0 + n, :, :])

        def xi_scalar(h, k):
            n = V_BLOCKS[h][k]
            if h == 1:
                n += G_BLOCKS
            if n < 4:
                xi_block(h, k, n, 4 - n, nc.scalar.copy)

        def xi_gpsimd(h, k):
            n = V_BLOCKS[h][k]
            v = x_raw[h][:, k, :, :].rearrange("p j (m t) -> p t m j", t=4)
            for t in range(n, n + G_BLOCKS):
                nc.gpsimd.tensor_scalar(
                    out=xi[h][:, k, t, :, :], in0=v[:, t], scalar1=1.0, scalar2=0.0, op0=MULT, op1=ADD
                )

        def xi_vector(h, k):
            n = V_BLOCKS[h][k]
            if n % 2:
                xi_block(h, k, n - 1, 1, nc.vector.tensor_copy)
                n -= 1
            if n:
                xi_block(h, k, 0, n, nc.vector.tensor_copy)

        def x_quant(h, k):
            nc.vector.quantize_mx(
                out=xq[:, k, 512 * h : 512 * h + 512].bitcast(FP8X4),
                scales=xs[:, k, 512 * h : 512 * h + 512],
                in_=xi[h][:, k, :, :, :].rearrange("p t m j -> p (t m j)"),
            )

        def x_transpose(h, k, jp):
            words = x_raw[h][:].rearrange("p k j w -> p (k j w)").bitcast(F32)
            b = bank("xt%d%d%d" % (h, k, jp), [P, 2, 2, P])
            for jj in range(2):
                base = (4 * k + 2 * jp + jj) * 256
                for u in range(2):
                    nc.tensor.transpose(b[:, jj, u, :], words[:, base + u : base + 256 : 2], ident[:])
            return b

        def x_empty(h, k, jp, b):
            words = x_t[:].rearrange("m a c t -> m (a c t)").bitcast(F32)
            base = (1024 * h + 512 * k) * 2
            dst = words[:, base : base + 1024].rearrange("m (p j u) -> m p j u", j=4, u=2)
            nc.scalar.copy(out=dst[:, :, 2 * jp : 2 * jp + 2, :], in_=b[:].rearrange("m j u p -> m p j u"))

        def keep_busy(name, n, words, scales, k, cols):
            b = bank(name, [P, 512])
            for i in range(n):
                nc.tensor.matmul_mx(
                    out=b[:],
                    lhsT=a_0[:].bitcast(FP4X4),
                    lhsT_scale=a_s[:, 0, 0:P],
                    rhs=words[:, k, cols : cols + 512].bitcast(FP8X4),
                    rhs_scale=scales[:, k, cols : cols + 512],
                    start=True,
                    stop=True,
                )

        def s1_mm(h, ch):
            b = bank("s1_%d_%d" % (h, ch), [P, 4, P])
            for t in range(4):
                w = 512 * h + P * t
                for k in range(2):
                    nc.tensor.matmul_mx(
                        out=b[:, t, :],
                        lhsT=xq[:, k, w : w + P].bitcast(FP8X4),
                        lhsT_scale=xs[:, k, w : w + P],
                        rhs=a_w[:, k, 2 * P * ch : 2 * P * (ch + 1)].bitcast(FP4X4),
                        rhs_scale=a_s[:, k, P * ch : P * (ch + 1)],
                        start=(k == 0),
                        stop=(k == 1),
                    )
            return b

        def s1_add(h, ch, b):
            cols = slice(P * ch, P * (ch + 1))
            nc.vector.tensor_tensor(
                out=h1f[:, h, 64 * ch : 64 * ch + 64, :, :],
                in0=b[:].rearrange("m t (c e) -> m c t e", e=2),
                in1=x_t[:, h, cols, :].rearrange("m (c e) t -> m c t e", e=2),
                op=ADD,
            )

        h1_tmp = {}

        def s1_empty(h, ch, b):
            t = sb("t_%d_%d" % (h, ch), [P, P, 4], F32, tag="s", bufs=2)
            nc.scalar.copy(out=t[:], in_=b[:].rearrange("m t c -> m c t"))
            h1_tmp[h, ch] = t

        def s1_add_gp(h, ch):
            cols = slice(P * ch, P * (ch + 1))
            nc.gpsimd.tensor_tensor(out=h1f[:, h, cols, :], in0=h1_tmp[h, ch][:], in1=x_t[:, h, cols, :], op=ADD)

        h1b = {}

        def h1_round(h, ch):
            if h not in h1b:
                h1b[h] = sb("h1b%d" % h, [P, C, 4], BF16)
            dst = h1b[h][:, P * ch : P * (ch + 1), :].rearrange("m (c e) t -> m c e t", e=2)
            src = h1f[:, h, 64 * ch : 64 * ch + 64, :, :].rearrange("m c t e -> m c e t")
            if (h, ch) in G_RD:
                nc.gpsimd.tensor_scalar(out=dst, in0=src, scalar1=1.0, scalar2=0.0, op0=MULT, op1=ADD)
            else:
                nc.scalar.copy(out=dst, in_=src)

        def h1_quant(h, c0, n):
            nc.vector.quantize_mx(
                out=h1q[:, h, c0 : c0 + n].bitcast(FP8X4),
                scales=h1s[:, h, c0 : c0 + n],
                in_=h1b[h][:, c0 : c0 + n, :].rearrange("m c t -> m (c t)"),
            )

        def b_permute_gp(a, k, part):
            m0 = 16 * part
            for src, dst, w in ((b_raw, b_w, 2), (bs_raw, b_s, 1)):
                nc.gpsimd.tensor_copy(
                    out=dst[:, k, 512 * w * a : 512 * w * (a + 1)].rearrange("p (t m b) -> p t m b", t=4, b=w)[:, :, m0 : m0 + 16],
                    in_=src[:, k, 512 * w * a : 512 * w * (a + 1)].rearrange("p (m t b) -> p t m b", t=4, b=w)[:, :, m0 : m0 + 16],
                )

        def b_permute(a, part):
            if part == 0:
                nc.vector.tensor_copy(
                    out=b_w[:, :, 1024 * a : 1024 * a + 1024].rearrange("p k (t m b) -> p k t m b", t=4, b=2),
                    in_=b_raw[:, :, 1024 * a : 1024 * a + 1024].rearrange("p k (m t b) -> p k t m b", t=4, b=2),
                )
            else:
                nc.vector.tensor_copy(
                    out=b_s[:, :, 512 * a : 512 * a + 512].rearrange("p k (t m) -> p k t m", t=4),
                    in_=bs_raw[:, :, 512 * a : 512 * a + 512].rearrange("p k (m t) -> p k t m", t=4),
                )

        h2t = {}
        h2i = {}

        def s2_mm(a, hc, t):
            b = bank("s2_%d%d%d" % (a, hc, t), [P, 512])
            w = 512 * a + P * t
            for k in range(2):
                nc.tensor.matmul_mx(
                    out=b[:],
                    lhsT=b_w[:, k, 2 * w : 2 * w + 2 * P].bitcast(FP4X4),
                    lhsT_scale=b_s[:, k, w : w + P],
                    rhs=h1q[:, k, 512 * hc : 512 * hc + 512].bitcast(FP8X4),
                    rhs_scale=h1s[:, k, 512 * hc : 512 * hc + 512],
                    start=(k == 0),
                    stop=(k == 1),
                )
            return b

        z_tiles = {}

        def s2_add(a, hc, t, b):
            z_tiles[a, hc, t] = sb("z_%d%d%d" % (a, hc, t), [P, 512], F32, tag="z", bufs=3)
            nc.vector.tensor_tensor(
                out=z_tiles[a, hc, t][:].rearrange("m (c e) -> m c e", e=2),
                in0=b[:].rearrange("m (c e) -> m c e", e=2),
                in1=h1f[:, a, 256 * hc : 256 * hc + 256, t, :],
                op=ADD,
            )

        def h2_gain(a, hc, t):
            if a not in h2t:
                h2t[a] = sb("h2t%d" % a, [P, 4, 2, 512], BF16, tag="r2", bufs=2)
            if (a, hc, t) in G_HS:
                nc.gpsimd.tensor_scalar(
                    out=h2t[a][:, t, hc, :].rearrange("m (u p e) -> m u p e", u=2, e=2),
                    in0=z_tiles[a, hc, t][:].rearrange("m (p u e) -> m u p e", u=2, e=2),
                    scalar1=gain_f[:, a, t : t + 1], scalar2=0.0, op0=MULT, op1=ADD
                )
                return
            nc.scalar.activation(
                out=h2t[a][:, t, hc, :].rearrange("m (u p e) -> m u p e", u=2, e=2),
                in_=z_tiles[a, hc, t][:].rearrange("m (p u e) -> m u p e", u=2, e=2),
                func=mybir.ActivationFunctionType.Copy,
                scale=gain_f[:, a, t : t + 1],
            )

        def h2_transpose(a, hc, tp):
            words = h2t[a][:].rearrange("m t k c -> m (t k c)").bitcast(F32)
            b = bank("ht%d%d%d" % (a, hc, tp), [P, 2, 2, P])
            for tt in range(2):
                base = ((2 * tp + tt) * 2 + hc) * 256
                for u in range(2):
                    nc.tensor.transpose(b[:, tt, u, :], words[:, base + P * u : base + P * (u + 1)], ident[:])
            return b

        def h2_empty(a, hc, tp, b):
            if a not in h2i:
                h2i[a] = sb("h2i%d" % a, [P, 2, 512, 4], BF16, tag="r1", bufs=2)
            words = h2i[a][:].rearrange("p k g j -> p (k g j)").bitcast(F32)
            base = (hc * 512 + tp * 256) * 2
            nc.scalar.copy(
                out=words[:, base : base + 512].rearrange("p (t m u) -> p t m u", t=2, u=2),
                in_=b[:].rearrange("p t u m -> p t m u"),
            )

        def h2_quant(a, hc):
            nc.vector.quantize_mx(
                out=h2q[:, hc, 512 * a : 512 * a + 512].bitcast(FP8X4),
                scales=h2s[:, hc, 512 * a : 512 * a + 512],
                in_=h2i[a][:, hc, :, :].rearrange("p g j -> p (g j)"),
            )

        def s3_mm(a, i, ks=(0, 1), b=None):
            if b is None:
                b = bank("s3_%d_%d" % (a, i), [P, 512])
            for k in ks:
                nc.tensor.matmul_mx(
                    out=b[:],
                    lhsT=e_w[:, k, 2 * P * i : 2 * P * (i + 1)].bitcast(FP4X4),
                    lhsT_scale=e_s[:, k, P * i : P * (i + 1)],
                    rhs=h2q[:, k, 512 * a : 512 * a + 512].bitcast(FP8X4),
                    rhs_scale=h2s[:, k, 512 * a : 512 * a + 512],
                    start=(k == 0),
                    stop=(k == 1),
                )
            return b

        o_tiles = {}
        s_tiles = {}

        def y_cols(n):
            a, i = divmod(n, 16)
            return y_sb[:, i, 512 * a : 512 * a + 512].rearrange("p (m t) -> p m t", t=4)

        def out_add(n, b):
            o_tiles[n] = sb("o_%d" % n, [P, P, 4], F32, tag="o", bufs=O_BUFS)
            nc.vector.tensor_tensor(out=o_tiles[n][:], in0=b[:].rearrange("p (t m) -> p m t", t=4), in1=y_cols(n), op=ADD)

        def out_empty(n, b):
            s_tiles[n] = sb("s_%d" % n, [P, P, 4], F32, tag="s", bufs=2)
            nc.scalar.copy(out=s_tiles[n][:], in_=b[:].rearrange("p (t m) -> p m t", t=4))

        def out_add_gp(n):
            o_tiles[n] = sb("g_%d" % n, [P, P, 4], F32, tag="g", bufs=3)
            nc.gpsimd.tensor_tensor(out=o_tiles[n][:], in0=s_tiles[n][:], in1=y_cols(n), op=ADD)

        def store(n):
            a, i = divmod(n, 16)
            nc.sync.dma_start(
                out=out[P * i : P * (i + 1), 512 * a : 512 * a + 512], in_=o_tiles[n][:].rearrange("p m t -> p (m t)")
            )

        banks = {}
        done = set()
        live = [0]

        def pe(name, needs, fn, *args):
            def go():
                banks[name] = fn(*args)
                live[0] += 1
            return (name, needs, go, True)

        def use(name, needs, src, fn, *args):
            def go():
                fn(*(args + (banks[src],)))
                live[0] -= 1
            return (name, needs + [src], go, False)

        def do(name, needs, fn, *args):
            return (name, needs, lambda: fn(*args), False)

        q_pe, q_v, q_s, q_g, q_d = [], [], [], [], []
        H = range(2)
        for h in H:
            for k in H:
                pass

        def PE_tr(h):
            return [pe(("tr", h, k, jp), [], x_transpose, h, k, jp) for k in H for jp in H]

        def PE_s1(h, chs):
            return [pe(("s1", h, ch), [("xq", h, 0), ("xq", h, 1)], s1_mm, h, ch) for ch in chs]

        def PE_s2(a, hc, ts=range(4)):
            return [pe(("s2", a, hc, t), [("q1", 0, hc), ("q1", 1, hc), ("bp", a, 0), ("bp", a, 1)], s2_mm, a, hc, t) for t in ts]

        def PE_ht(a, hc):
            return [pe(("ht", a, hc, tp), [("hs", a, hc, 2 * tp), ("hs", a, hc, 2 * tp + 1)], h2_transpose, a, hc, tp) for tp in H]

        def PE_s3a(ns):
            return [pe(("s3a", n), [("q2", n // 16, 0)], s3_mm, n // 16, n % 16, (0,)) for n in ns]

        def PE_s3b(ns):
            def fin(n):
                banks[("s3", n)] = s3_mm(n // 16, n % 16, (1,), banks[("s3a", n)])

            return [do(("s3", n), [("s3a", n), ("q2", n // 16, 1)], fin, n) for n in ns]

        def PE_s3(ns):
            return [pe(("s3", n), [("q2", n // 16, 0), ("q2", n // 16, 1)], s3_mm, n // 16, n % 16) for n in ns]

        def V_x(h, k):
            return [do(("xi", h, k), [], xi_vector, h, k), do(("xq", h, k), [("xi", h, k), ("xis", h, k)] + ([("xig", h, k)] if h == 1 and G_BLOCKS else []), x_quant, h, k)]

        def V_tt(h, chs):
            return [use(("tt", h, ch), [("xe", h, ch // 4, 0), ("xe", h, ch // 4, 1)], ("s1", h, ch), s1_add, h, ch) for ch in chs if (h, ch) not in G_ADD]

        def S_a1(h, ch):
            return [use(("sa", h, ch), [], ("s1", h, ch), s1_empty, h, ch)] if (h, ch) in G_ADD else []

        def G_a1(h, ch):
            return [do(("tt", h, ch), [("sa", h, ch), ("xe", h, ch // 4, 0), ("xe", h, ch // 4, 1)], s1_add_gp, h, ch)] if (h, ch) in G_ADD else []

        def G_xi(h, k):
            return [do(("xig", h, k), [], xi_gpsimd, h, k)] if G_BLOCKS else []


        def V_q1(h, hc):
            if h == 0:
                if hc == 0:
                    return []
                return [
                    do(("q1", 0, 1), [("rd", h, ch) for ch in range(8)], h1_quant, 0, 0, C),
                    do(("q1", 0, 0), [("q1", 0, 1)], lambda: None),
                ]
            return [do(("q1", h, hc), [("rd", h, ch) for ch in range(4 * hc, 4 * hc + 4)], h1_quant, h, 512 * hc, 512)]

        def V_bp(a, k):
            if (a, k) in G_BP:
                return []
            return [do(("bp", a, k), [], b_permute, a, k)]

        def V_st(a, hc, ts=range(4)):
            return [use(("st", a, hc, t), [("tt", a, ch) for ch in range(4 * hc, 4 * hc + 4)], ("s2", a, hc, t), s2_add, a, hc, t) for t in ts]

        def V_q2(a, hc):
            return [do(("q2", a, hc), [("he", a, hc, 0), ("he", a, hc, 1)], h2_quant, a, hc)]

        def V_o(ns):
            return [use(("o", n), [], ("s3", n), out_add, n) for n in ns if n not in G_OUT]

        def G_bp(a, k):
            return [do(("bpp", a, k, j) if j < 7 else ("bp", a, k), [], b_permute_gp, a, k, j) for j in range(8)] if (a, k) in G_BP else []

        def S_xi(h, k):
            return [do(("xis", h, k), [], xi_scalar, h, k)]

        def S_xe(h, k):
            return [use(("xe", h, k, jp), [], ("tr", h, k, jp), x_empty, h, k, jp) for jp in H]

        def S_rd(h, chs):
            return [do(("rd", h, ch), [("tt", h, ch)], h1_round, h, ch) for ch in chs]

        def S_hs(a, hc, ts=range(4)):
            return [do(("hs", a, hc, t), [("st", a, hc, t)], h2_gain, a, hc, t) for t in ts]

        def S_he(a, hc):
            return [use(("he", a, hc, tp), [], ("ht", a, hc, tp), h2_empty, a, hc, tp) for tp in H]

        def S_o(ns):
            return [use(("os", n), [("o", p) for p in G_OUT if p < n and sum(1 for z in G_OUT if p < z < n) >= 1], ("s3", n), out_empty, n) for n in ns if n in G_OUT]

        def G_o(ns):
            return [do(("o", n), [("os", n)], out_add_gp, n) for n in ns if n in G_OUT]

        def W1(n):
            return [do(("w1",), [("xq", 0, 0)], keep_busy, "w1", n, xq, xs, 0, 0)]

        def W2(n):
            return [do(("w2",), [("xq", 1, 0)], keep_busy, "w2", n, xq, xs, 1, 0)]

        def W3(n):
            return [do(("w3",), [("q1", 1, 0)], keep_busy, "w3", n, h1q, h1s, 1, 0)]

        q_pe += PE_tr(0) + W1(3) + PE_s1(0, range(4)) + PE_tr(1) + PE_s1(0, range(4, 8)) + PE_s1(1, range(8))
        q_pe += W2(4) + PE_s2(0, 0) + PE_s2(0, 1) + PE_ht(0, 0) + W3(3) + PE_ht(0, 1) + PE_s3a(range(6))
        q_pe += PE_s3b((0, 1)) + PE_s2(1, 0, (0,)) + PE_s3b((2,)) + PE_s2(1, 0, (1,)) + PE_s3b((3,)) + PE_s2(1, 0, (2,)) + PE_s3b((4,)) + PE_s2(1, 0, (3,))
        q_pe += PE_s3b((5,)) + PE_s2(1, 1, (0,)) + PE_s3((6,)) + PE_ht(1, 0) + PE_s2(1, 1, (1,)) + PE_s3((7, 8)) + PE_s2(1, 1, (2,)) + PE_s3((9,))
        q_pe += PE_s2(1, 1, (3,)) + PE_s3((10, 11, 12)) + PE_ht(1, 1) + PE_s3(range(13, 32))

        q_v += V_x(0, 0) + V_x(0, 1) + V_tt(0, range(3)) + V_x(1, 0) + V_tt(0, range(3, 4)) + V_x(1, 1) + V_bp(0, 0) + V_tt(0, range(4, 6)) + V_bp(0, 1) + V_tt(0, range(6, 8))
        q_v += V_tt(1, (0, 1, 2, 3)) + V_q1(0, 0) + V_q1(0, 1) + V_tt(1, (4, 5)) + V_q1(1, 0)
        q_v += V_tt(1, (6, 7))
        q_v += V_st(0, 0, (0, 1)) + V_q1(1, 1) + V_st(0, 0, (2, 3)) + V_st(0, 1) + V_q2(0, 0) + V_bp(1, 0) + V_q2(0, 1) + V_bp(1, 1)
        q_v += V_o((0, 1)) + V_st(1, 0, (0,)) + V_o((2,)) + V_st(1, 0, (1,)) + V_o((3,)) + V_st(1, 0, (2,)) + V_o((4,)) + V_st(1, 0, (3,)) + V_o((5,))
        q_v += V_st(1, 1, (0,)) + V_o((6,)) + V_st(1, 1, (1,)) + V_o((7,)) + V_q2(1, 0) + V_o((8,)) + V_st(1, 1, (2,)) + V_o((9,)) + V_st(1, 1, (3,))
        q_v += V_o((10, 11, 12)) + V_q2(1, 1) + V_o(range(13, 32))

        def HS(a, hc, ts=range(4)):
            return S_hs(a, hc, [t for t in ts if (a, hc, t) not in G_HS])

        q_s += S_xi(0, 0) + S_xi(0, 1) + S_xe(0, 0) + S_xe(0, 1) + S_xi(1, 0) + S_xi(1, 1)
        seq = [(0, n) for n in range(8)] + [(1, n) for n in range(8)]
        late = []
        for j, (h, ch) in enumerate(seq):
            if (h, ch) in G_RD:
                pass
            elif (h, ch) in G_ADD:
                late = S_rd(h, (ch,))
            else:
                q_s += S_rd(h, (ch,)) + late
                late = []
            if (h, ch) == (0, XE_AT):
                q_s += S_xe(1, 0) + S_xe(1, 1)
            if j + 2 < 16:
                q_s += S_a1(*seq[j + 2])
        q_s += late
        q_s += HS(0, 0) + HS(0, 1, (0, 1)) + S_he(0, 0) + HS(0, 1, (2, 3)) + S_he(0, 1) + S_o(range(0, 3)) + HS(1, 0, (0, 1)) + S_o((3, 4)) + HS(1, 0, (2,)) + HS(1, 0, (3,)) + S_o((5,)) + S_he(1, 0) + S_o((6,))
        q_s += HS(1, 1, (0, 1)) + S_o((7, 8, 9)) + HS(1, 1, (2, 3)) + S_o((10, 11)) + S_he(1, 1) + S_o(range(12, 32))
        q_g += G_xi(1, 0) + G_xi(1, 1)
        for h in H:
            for n in range(8):
                q_g += G_a1(h, n) + (S_rd(h, (n,)) if (h, n) in G_RD else [])
        for a in H:
            for hc in H:
                for t in range(4):
                    q_g += S_hs(a, hc, (t,)) if (a, hc, t) in G_HS else []
        q_g += G_o(range(32))
        order = sorted(range(32), key=lambda n: n + (G_LAG if n in G_OUT else 0))
        q_d += [do(("w", n), [("o", n)], store, n) for n in order]

        queues = [q_pe, q_v, q_s, q_g, q_d]
        while any(queues):
            moved = False
            for q in queues:
                while q and all(n in done for n in q[0][1]) and not (q[0][3] and live[0] >= 8):
                    name, needs, go, isbank = q.pop(0)
                    go()
                    done.add(name)
                    moved = True
            assert moved, [q[0][:2] for q in queues if q]
